import numpy as np, ml_dtypes
CORES = [24,25,26,27,28,29,30,31]
N = 8
BF = ml_dtypes.bfloat16
def gentries(a):
    return np.ascontiguousarray(a.reshape(8, 16, -1).transpose(0, 2, 1)).reshape(8, -1)
def gtable(e):
    e = np.asarray(e); return np.ascontiguousarray(e.reshape(8, -1, 16).transpose(0, 2, 1)).reshape(128, -1).astype(np.int32)
V, G, D, S, RO = 1024, 512, 4, 4, 3
def parts(rng):
    o = np.argsort(rng.random((N, 8, V)), axis=2); pos = np.argsort(o, axis=2)
    x = rng.integers(0, 256, (N, 8, 16, 1)) + np.add.accumulate(rng.integers(-100, 101, (N, 8, 16, V)), axis=3)
    phi = np.take_along_axis(x, pos[:, :, None, :], 3) & 255
    nb = np.stack([np.take_along_axis(o, (pos + j) % V, 2) for j in (-1, 1, -32, 32)[:D]], 2)
    snd = np.argsort(rng.random((N, 8, V)), axis=2)[..., :G]
    return phi, nb, np.ascontiguousarray(snd)
def mix(rng, nb, own, ghost):
    z = rng.random(nb.shape)
    nb = np.where(z < ghost, rng.integers(V, V + G, nb.shape), np.where(z < ghost + own, rng.integers(0, V, nb.shape), nb))
    return np.take_along_axis(nb, np.argsort(rng.random(nb.shape), axis=2), 2)
def pack(phi, nb, snd):
    return {"phi": np.ascontiguousarray(phi.reshape(N, 128, V)).astype(np.float32).astype(BF), "nb": np.ascontiguousarray(nb.reshape(N, 8, D * V)).astype(np.int32),
            "snd": np.stack([gtable(a) for a in snd])}
def setup_inputs(rng):
    phi, nb, snd = parts(rng)
    own = rng.choice(np.array([0.0, 0.05, 0.15, 0.3]), (N, 8, 1, 1)); ghost = rng.choice(np.array([0.02, 0.05, 0.1, 0.2]), (N, 8, 1, 1))
    return pack(phi, mix(rng, nb, own, ghost), snd)
def setup_inputs_chains(rng):
    phi, nb, snd = parts(rng); v = np.arange(V); lens = [S, S + 1, S + 2, 2 * S + 1, 3 * S, S * S + 1, V, 5]
    steep = rng.random((N, 8, 16, 1)) < 0.5; steep[np.arange(N), (6 - np.arange(N)) % 8, :8] = True
    step = np.where(steep, rng.choice(np.array([-1, 1]), (N, 8, 16, 1)) * rng.integers(100, 128, (N, 8, 16, V)), rng.integers(-100, 101, (N, 8, 16, V)) + rng.integers(-27, 28, (N, 8, 16, 1)))
    phi = (rng.integers(0, 256, (N, 8, 16, 1)) + np.add.accumulate(step, axis=3)) & 255
    for q in range(N):
        for g in range(8):
            b = lens[(g + q) % 8]; head = v - v % b
            down = np.maximum(v - 1, head); up = np.minimum(np.minimum(v + 1, head + b - 1), V - 1)
            nb[q, g] = np.stack([down, up, v, down][:D])
            h = v[v % b == 0][1::2]; nb[q, g, D - 1, h] = rng.integers(V, V + G, len(h))
    return pack(phi, mix(rng, nb, 0.0, 0.0), snd)
def steep_sums(rng, n):
    return np.concatenate([np.zeros((16, 1), np.int64), np.add.accumulate(rng.integers(122, 128, (16, n)), axis=1)], axis=1)
def deep(rng, phi, nb, snd, g):
    T = S * (S + 1); t = np.arange(T + 1); root = t % (S + 1) == 0; slot = rng.integers(0, G, N); last = np.zeros((N, 16, 1), np.int64)
    sign = np.where(np.argsort(rng.random((N, 16, 1)), axis=1) < 8, 1, -1)
    for q in range(N):
        w = np.sort(rng.permutation(V // 2)[:T + 1]); a = np.zeros(T + 1, np.int64)
        a[root] = w[:S + 1]; a[~root] = w[S + 1:]
        y = rng.integers(0, 256, (16, 1)) + sign[q] * steep_sums(rng, T)
        phi[q, g][:, a] = y & 255; last[q] = y[:, T:] & 255
        lo = np.concatenate([a[:1], a[:-1]]); nb[q, g][:, a] = np.stack([lo, a, lo, a][:D]); snd[q, g, slot[q]] = a[T]
    for q in range(N):
        w = V // 2 + np.sort(rng.permutation(V // 2)[:(S + 1) * (S + 1)]); o = (q - 1) % N
        b = np.zeros(T + 1, np.int64); b[0] = V + slot[o]
        b[1:][root[1:]] = np.concatenate([w[:S - 1], w[2 * S:2 * S + 1]]); b[1:][~root[1:]] = w[2 * S + 1:]
        y = last[o] + sign[o] * steep_sums(rng, T); phi[q, g][:, b[1:]] = y[:, 1:] & 255
        nb[q, g][:, b[1:]] = np.stack([b[:-1], b[1:], b[:-1], b[1:]][:D])
        z = w[S - 1:2 * S]; y = rng.integers(0, 256, (16, 1)) - sign[o] * steep_sums(rng, S); phi[q, g][:, z] = y & 255
        lo = np.concatenate([z[S:], z[:-1]]); hi = np.concatenate([z[S:], z[1:S], b[T:]])
        nb[q, g][:, z] = np.stack([lo, hi, lo, hi][:D])
def late(rng, nb, g):
    J = 3 * S; F = J + 2; P = S * S + S + 1; M = 3 * F + P + 4; j = np.arange(F)
    path = np.concatenate([np.array([J - 1]), 3 * F + np.arange(S), 3 * F + np.arange(S + 1, P), np.array([M - 1])])
    lo = np.arange(M); hi = np.arange(M)
    lo[:F] = F + j; hi[:F] = F + j; lo[J:F] = j[J:]
    lo[F:2 * F] = j; hi[F + 1:2 * F] = 2 * F + j[:-1]; lo[2 * F:3 * F] = j
    lo[path[1:]] = path[:-1]
    c = 3 * F + S; lo[c] = M - 4; hi[c] = M - 4; lo[M - 4] = M - 1; hi[M - 4] = M - 1
    lo[M - 3] = M - 2; hi[M - 3] = M - 2; lo[M - 2] = M - 3; hi[M - 2] = M - 1
    for q in range(N):
        w = np.sort(rng.permutation(V)[:M]); nb[q, g][:, w] = np.stack([w[lo], w[hi], w[lo], w[hi]][:D])
def setup_inputs_loops(rng):
    phi, nb, snd = parts(rng); nb = mix(rng, nb, 0.1, rng.choice(np.array([0.02, 0.05, 0.1]), (N, 8, 1, 1)))
    far = S * S; J = min(S + 2, V // (1 + S + far)); M = J * (1 + S + far)
    ids = np.sort(np.argsort(rng.random((N, 8, V)), axis=2)[..., :M], axis=2)
    j = np.arange(J).reshape(J, 1); br = J + S * j + np.arange(S); pa = J + J * S + far * j + np.arange(far)
    lo = np.concatenate([br[:, S - 1], np.concatenate([j, br[:, :-1]], axis=1).reshape(-1), np.concatenate([j, pa[:, :-1]], axis=1).reshape(-1)])
    hi = np.arange(M); hi[:J] = br[:, S - 1]; hi[br[1:, S - 1]] = pa[:-1, far - 1]
    step = rng.choice(np.array([-1, 1]), (N, 8, 16, 1, 1)) * rng.integers(120, 128, (N, 8, 16, J, S + far)); a = rng.integers(0, 256, (N, 8, 16, J, 1))
    xb = a - np.add.accumulate(step[..., :S], axis=4); xp = a + np.add.accumulate(step[..., S:], axis=4)
    x = np.concatenate([a.reshape(N, 8, 16, J), xb.reshape(N, 8, 16, J * S), xp.reshape(N, 8, 16, J * far)], axis=3) & 255
    for q in range(N):
        for g in (0, 1, 3, 4, 6, 7):
            w = ids[q, g]; phi[q, g][:, w] = x[q, g]
            nb[q, g][:, w] = np.stack([w[lo], w[hi], w[lo], w[hi]][:D])
    deep(rng, phi, nb, snd, 2); late(rng, nb, 5)
    return pack(phi, mix(rng, nb, 0.0, 0.0), snd)
def setup_inputs_ties(rng):
    phi, nb, snd = parts(rng); v = np.arange(V)
    t = rng.choice(np.array([0, 1, 127, 128, 129, 255]), (N, 8, 16, 6)); phi = np.take_along_axis(t, rng.integers(0, 6, (N, 8, 1, V)), 3)
    nb = mix(rng, nb, 0.2, rng.choice(np.array([0.0, 0.05, 0.15]), (N, 8, 1, 1)))
    nb[:, 1::2, 1] = nb[:, 1::2, 0]; nb[:, 2, 0] = v
    nb[:, 4] = np.minimum(v + rng.integers(0, 5, (N, D, V)), V - 1)
    return pack(phi, nb, snd)
def setup_inputs_ring(rng):
    phi, nb, snd = parts(rng)
    share = np.stack([rng.permutation(np.array([0.0, 0.0, 0.3, 0.3, 0.7, 0.7, 1.0, 1.0])) for q in range(N)]).reshape(N, 8, 1, 1)
    nb = mix(rng, nb, 0.1 * (share < 0.9), share)
    snd[:, ::2] = rng.choice(np.array([0, V - 1, V // 2, 3]), (N, 4, G)); snd[:, 1, 0] = 0; snd[:, 1, G - 1] = V - 1
    nb[:, 3] = rng.choice(np.array([0, V - 1, V, V + G - 1]), (N, D, V))
    top = V - V // 16; snd[:, 5] = rng.integers(top, V, (N, G))
    high = np.where(rng.random((N, D, V)) < 0.5, rng.integers(V, V + G, (N, D, V)), rng.integers(top, V, (N, D, V)))
    nb[:, 5] = np.where(np.arange(V) < top, high, rng.integers(0, 16, (N, D, V)))
    return pack(phi, nb, snd)
def setup_inputs_spread(rng):
    phi, nb, snd = parts(rng)
    phi = np.minimum((np.exp2(8 * rng.random((N, 8, 1, V))) * rng.random((N, 8, 16, V))).astype(np.int64), 255)
    hub = np.minimum(((V + G) * rng.random(nb.shape) ** 3).astype(np.int64), V + G - 1)
    nb = mix(rng, np.where(rng.random(nb.shape) < rng.choice(np.array([0.1, 0.3, 0.6]), (N, 8, 1, 1)), hub, nb), 0.0, 0.05)
    snd = np.minimum((V * rng.random((N, 8, G)) ** 2).astype(np.int64), V - 1)
    return pack(phi, nb, snd)
def check_inputs(d):
    bad = []
    for k, lo, hi in (("phi", 0, 255), ("nb", 0, V + G - 1), ("snd", 0, V - 1)):
        a = np.asarray(d[k]).astype(np.float64)
        if not (np.min(a) >= lo and np.max(a) <= hi): bad.append("range of " + k)
    a = np.asarray(d["phi"]).astype(np.float64)
    if not np.all(a == np.floor(a)): bad.append("whole numbers in phi")
    return bad
def narrow(t, ix):
    return np.take_along_axis(t, ix, 2)
def broad(t, ix):
    return np.take_along_axis(t, ix[:, :, None, :], 3)
def absolute(r, k, gk, gb):
    gh = r >= V; c = np.where(gh, r - V, 0)
    return k + np.where(gh[:, :, None, :], broad(gk, c), 0), np.where(gh, narrow(gb, c), N * r + np.arange(N).reshape(N, 1, 1))
def reference(phi, nb, snd):
    p = phi.astype(np.float32).astype(np.int64).reshape(N, 8, 16, V); nbl = nb.astype(np.int64).reshape(N, 8, D, V)
    sl = np.stack([gentries(a) for a in snd]).astype(np.int64); before = (np.arange(N) - 1) % N
    own = np.zeros((N, 8, V), np.int64) + np.arange(V); slot = np.zeros((N, 8, G), np.int64) + np.arange(V, V + G)
    num = N * own + np.arange(N).reshape(N, 1, 1); none = np.zeros((N, 8, 16, G), np.int64); BIG = 2 ** 40
    r, k, s = own.copy(), np.zeros((N, 8, 16, V), np.int64), own.copy(); ks, b = k.copy(), num.copy()
    gp = broad(p, sl)[before]
    for rnd in range(RO):
        gk, gb = broad(ks, sl)[before], narrow(b, sl)[before]
        ks, b = absolute(r, k, gk, gb)
        uw = np.concatenate([p + 256 * ks, gp + 256 * gk], axis=3); bw = np.concatenate([b, gb], axis=2)
        rw = np.concatenate([r, slot], axis=2); kw = np.concatenate([k, none], axis=3); sw = np.concatenate([ks, gk], axis=3)
        us = broad(uw, s); cj = np.full((N, 8, V), BIG); cw = cj.copy(); uj = np.zeros((N, 8, V), np.int64); ww = uj.copy()
        for i in range(D):
            u = narrow(nbl[:, :, i], s); c = np.add.reduce(np.abs(broad(uw, u) - us), axis=2)
            t = (narrow(bw, u) < num) & (c < cj); cj = np.where(t, c, cj); uj = np.where(t, u, uj)
            t = (narrow(rw, u) == own) & (c < cw); cw = np.where(t, c, cw); ww = np.where(t, u, ww)
        root = r == own; join = root & (cj < BIG)
        o = ((broad(uw, uj) - us + 128) >> 8) + broad(kw, uj) - broad(sw, uj)
        pw = np.concatenate([np.where(join, narrow(rw, uj), r), slot], axis=2)
        ow = np.concatenate([np.where(join[:, :, None, :], o, k), none], axis=3)
        s = np.where(root & ~join & (cw < BIG), ww, s)
        r, k = own.copy(), np.zeros((N, 8, 16, V), np.int64)
        for step in range(S):
            k = k + broad(ow, r); r = narrow(pw, r)
        ks, b = absolute(r, k, gk, gb)
    return {"yk": ks.reshape(N, 128, V).astype(np.float32), "yr": b.astype(np.float32)}

@@ -1,0 +1,587 @@
+from concourse.mybir import AluOpType, ActivationFunctionType
+
+F, H16, I32, U16, F16 = "float32", "bfloat16", "int32", "uint16", "float16"
+SCRATCH = {}
+for _d, _l in (
+    (U16, "SNL 32 SGL 64 NL1 256 NL3 256 UL 64 PL 64 P2L 64 RL 64 QL 32 SL 64 YL 64"),
+    (I32, "SNI 32 NBI 1024 PI 16 CI 128"),
+    (F16, "NBS 1024 LM 512"),
+    (H16, "PHI 1536 PSG 1024 PS2 1024 HI 1536 SC1 1536 SC2 1536 SC3 1536 SCN 1536 TMP 1024 WK2 1536 WK3 1536 RR 1536 "
+          "PR 1536 P2R 1536 OT 1536 OB 1024 O2 1536 O2B 1024 HT 1536 KB 1024 SBR 512 O2S 512 P2S 512 S1 1024 S2 1024 "
+          "S3 1024 M1 4096 KG 4096 BF 1024"),
+    (F, "YP 1024 YSG 1024 YT 2560 XT 1536 MM 4096 YK 1024 YR 1024"),
+    (H16, "MKI 512 MK 512 RNB 64 RU 32 R2 64 IDB 128 IDS 128 Z 144 W4 128 W5 128 W5N 128 A03 128 A45 128 A09 128 "
+          "WQ 128 WB 192"),
+    (F, "PC 48 ROW 144 GB 128 OH 16 STB 12 ONE 128 R2T 64 R2A 64 R2B 64 PERM 128 WA 192 WT 192 WM2 8 XN 128"),
+    (F, "PEN 256 PU 256 CP 256 T1 128 M2 128 TD 128 U2 128 SM 1024 LA 128 LB 128 LE 128 LH 128 WN 64"),
+):
+    _w = _l.split()
+    for _k in range(0, len(_w), 2):
+        SCRATCH[_w[_k]] = ("sbuf", [128, int(_w[_k + 1])], _d)
+for _n in ("pC", "pD", "pE", "pU", "pX", "pY0", "pY1", "pW"):
+    SCRATCH[_n] = ("psum", [128, 512], F)
+SEMAPHORES = ["cV", "cA", "cP", "cG", "sent", "a0", "a1", "a2", "b0", "b1", "b2"] + ["d%d" % k for k in range(24)]
+
+AL = AluOpType
+AF = ActivationFunctionType
+ADD, SUB, MUL, MAX, MIN, LT, GE, EQ = AL.add, AL.subtract, AL.mult, AL.max, AL.min, AL.is_lt, AL.is_ge, AL.is_equal
+BIG = float(2 ** 22)
+BIG1 = float(2 ** 26)
+MID1 = 2040.0 * 8192.0
+DEF1 = 16719872.0
+LIFT = 192.0 + 1.0 / 512
+ROUND16 = 1.5 * 2 ** 27
+
+
+def _emit(g, T, ops):
+    queue = {"V": g.vector, "A": g.scalar, "P": g.tensor, "G": g, "S": g.sync}
+    cnt = {"V": "cV", "A": "cA", "P": "cP", "G": "cG"}
+
+    def meet(x, y):
+        return x[0] == y[0] and x[1] < y[2] and y[1] < x[2]
+
+    known = {q: {} for q in queue}
+    clock, waits, used, touch = [], [], set(), {}
+    for n, o in enumerate(ops):
+        q = o["q"]
+        if q == "X":
+            clock.append({})
+            waits.append([])
+            touch.setdefault(o["w"][0][0], []).append(n)
+            continue
+        deps = []
+        names = set(x[0] for x in o["r"] + o["w"])
+        for m in sorted(set(m for x in names for m in touch.get(x, []))):
+            p = ops[m]
+            if p["q"] == "P" and q == "P":
+                continue
+            hit = any(meet(x, y) for x in o["r"] + o["w"] for y in p["w"]) or any(meet(x, y) for x in o["w"] for y in p["r"])
+            if not hit and p["q"] != q:
+                hit = any(x[0] == y[0] and x[0][0] == "p" for x in o["r"] + o["w"] for y in p["r"] + p["w"])
+            if hit:
+                deps.append(m)
+        mine = []
+        for m in reversed(deps):
+            key = ops[m]["q"] if ops[m]["own"] is None else ("own", m)
+            if known[q].get(key, -1) >= m:
+                continue
+            mine.append(m)
+            used.add(m)
+            known[q][key] = m
+            for kk, vv in clock[m].items():
+                if known[q].get(kk, -1) < vv:
+                    known[q][kk] = vv
+        waits.append(mine)
+        for x in names:
+            touch.setdefault(x, []).append(n)
+        clock.append(dict(known[q]))
+    val, num = {}, {q: 0 for q in cnt}
+    for n, o in enumerate(ops):
+        if o["own"] is not None:
+            val[n] = o["own"]
+        elif n in used:
+            num[o["q"]] += 1
+            val[n] = (cnt[o["q"]], num[o["q"]])
+    for n, o in enumerate(ops):
+        if o["q"] == "X":
+            continue
+        for m in waits[n]:
+            queue[o["q"]].wait_ge(T.sem[val[m][0]], val[m][1])
+        ins = o["f"]()
+        if o["inc"] and n in val:
+            ins.then_inc(T.sem[val[n][0]], 1 if o["own"] is None else 16)
+    final = {}
+    for n in val:
+        final[val[n][0]] = max(final.get(val[n][0], 0), val[n][1])
+    for s in final:
+        g.wait_ge(T.sem[s], final[s])
+
+
+def rank_program(g, core, T, topo):
+    rank = T.rank_of(core)
+    if rank is None:
+        return
+    nr = len(T.cores)
+    nxt = T.cores[(rank + 1) % nr]
+    prv = T.cores[(rank - 1) % nr]
+    ops = []
+    ndma = [0]
+    nsent = [0]
+
+    def v(name, a=0, b=None, s=1, rows=None):
+        b = T[name].shape[1] if b is None else b
+        ap = T[name][:, a:b:s] if rows is None else T[name][rows[0]:rows[1]:rows[2], a:b:s]
+        return (ap, [(name, a, b)])
+
+    def ind(win, off):
+        return (win[0].indirect(off[0]), win[1] + off[1])
+
+    def part(name, n, h):
+        return v(name, n * h, n * h + n)
+
+    def sm(k):
+        return part("SM", 64, k)
+
+    def pc(k):
+        return part("PC", 1, k)
+
+    def oh(k):
+        return part("OH", 1, k)
+
+    def rec(q, f, w, r, own=None, inc=True):
+        ops.append({"q": q, "f": f, "w": [x for a in w for x in a[1]], "r": [x for a in r for x in a[1]], "own": own, "inc": inc})
+
+    def val(s):
+        return s[0] if isinstance(s, tuple) else s
+
+    def aps(*s):
+        return [x for x in s if isinstance(x, tuple)]
+
+    def cp(out, in_):
+        rec("V", lambda: g.vector.tensor_copy(out[0], in_[0]), [out], [in_])
+
+    def tt(out, a, b, op):
+        rec("V", lambda: g.vector.tensor_tensor(out[0], a[0], b[0], op), [out], [a, b])
+
+    def ts(out, a, s1, op0, s2=None, op1=None):
+        if op1 is None:
+            rec("V", lambda: g.vector.tensor_scalar(out[0], a[0], val(s1), None, op0), [out], [a] + aps(s1))
+        else:
+            rec("V", lambda: g.vector.tensor_scalar(out[0], a[0], val(s1), val(s2), op0, op1), [out], [a] + aps(s1, s2))
+
+    def ms(out, c):
+        rec("V", lambda: g.vector.memset(out[0], c), [out], [])
+
+    def act(out, in_, func=AF.Copy, bias=0.0, scale=1.0):
+        rec("A", lambda: g.scalar.activation(out[0], in_[0], func, bias=val(bias), scale=val(scale)), [out], [in_] + aps(bias, scale))
+
+    def lin(out, in_, scale, bias):
+        act(out, in_, AF.Identity, bias, scale)
+
+    def mul(out, in_, scale):
+        act(out, in_, AF.Copy, 0.0, scale)
+
+    def mm(out, l, r, start=True, stop=True):
+        rec("P", lambda: g.tensor.matmul(out[0], l[0], r[0], start, stop), [out], [l, r])
+
+    def mms(out, pairs, start=True, stop=True):
+        for j, (l, r) in enumerate(pairs):
+            mm(out, l, r, start and j == 0, stop and j == len(pairs) - 1)
+
+    def iota(out, pat, base, cm, flt=True):
+        if flt:
+            rec("G", lambda: g.iota(out[0], pat, base, cm, allow_small_or_imprecise_dtypes=True), [out], [])
+        else:
+            rec("G", lambda: g.iota(out[0], pat, base, cm), [out], [])
+
+    def asel(out, in_, pat, base, cm, op=EQ, fill=0.0):
+        rec("G", lambda: g.affine_select(out[0], in_[0], pat, op, fill, base, cm), [out], [in_])
+
+    def dma(q, out, in_):
+        e = g.sync if q == "S" else g.scalar
+        s = "d%d" % ndma[0]
+        ndma[0] += 1
+        rec(q, lambda: e.dma_start(out[0], in_[0]), [out], [in_], own=(s, 16))
+
+    def hbm(ap):
+        return (ap, [])
+
+    mask = topo.mask(core, nxt)
+    rid, pid, _ = topo.addr(nxt)
+
+    def send(sem, src, dst):
+        nsent[0] += len(topo.engines(core, nxt))
+        rec("G", lambda: g.remote_dma(T[dst][:, 1024:1536], src[0], T.sem[sem], T.sem["sent"], pid, rid, mask), [], [src],
+            own=("sent", nsent[0]), inc=False)
+
+    def arrive(sem, dst):
+        rec("X", None, [v(dst, 1024, 1536)], [], own=(sem, len(topo.engines(prv, core))))
+
+    def to_list(src, n, dst, col):
+        for i in range(16):
+            mm(v("pW", col, col + n), v("Z", 15 - i, 143 - i), v(src, i, 16 * n, 16), i == 0, i == 15)
+        return lambda: cp(v(dst, 0, n), v("pW", col, col + n))
+
+    def t_to_list(la, lb, col):
+        mms(v("pW", col, col + 64), [(v(la), v("R2A")), (v(lb), v("R2B"))])
+
+    def own(name):
+        return v(name, 0, 1024)
+
+    def ghost(name):
+        return v(name, 1024, 1536)
+
+    row = v("ROW", 0, 128)
+
+    def numbers(h):
+        lin(part("RR", 128, h), row, oh(1), part("STB", 1, h))
+
+    AND, SHR = AL.bitwise_and, AL.logical_shift_right
+    p = v("PI", 0, 1)
+    dma("A", own("PHI"), hbm(T.phi[:]))
+    dma("S", v("SNI"), hbm(T.snd[:]))
+    iota(p, [[0, 1]], 0, 1, False)
+    iota(v("ROW"), [[1, 144]], 0, 0)
+    iota(v("NBI", 512, 1024), [[0, 512]], 0, 0, False)
+    ms(v("NBI", 0, 256), 0)
+    ts(v("PI", 1, 2), p, 15, AND)
+    ts(v("PI", 2, 3), p, 4, SHR)
+    ts(v("PI", 3, 4), p, 1, AND)
+    cp(v("PC", 0, 4), v("PI", 0, 4))
+    ms(v("NBI", 256, 512), 0)
+    dma("S", v("NBI", rows=(0, 128, 4)), hbm(T.nb[:]))
+    ts(v("OH"), v("ROW", 0, 16), pc(1), EQ)
+    ts(v("PI", 5, 6), p, 7, AND)
+    ts(pc(4), oh(3), float(rank), MUL, oh(2), ADD)
+    ts(v("PI", 6, 7), p, 3, SHR, 1, AND)
+    ts(pc(9), pc(4), oh(4), ADD)
+    cp(v("PC", 5, 7), v("PI", 5, 7))
+    ts(v("STB"), v("ROW", 0, 12), oh(0), MUL, pc(9), ADD)
+    lin(pc(11), pc(2), 16.0, 5.0)
+    lin(pc(12), pc(2), 16.0, 6.0)
+    lin(pc(14), oh(0), 1024.0, oh(3))
+    lin(pc(16), oh(5), 16.0, oh(6))
+    mul(pc(35), oh(2), -MID1)
+    lin(pc(17), oh(1), 8.0, pc(14))
+    lin(pc(36), pc(16), -8192.0, pc(35))
+    mul(pc(15), oh(2), -16.0 * BIG1)
+    mul(pc(37), pc(17), BIG1)
+    mul(pc(38), oh(4), 2048.0)
+    for h in range(8):
+        numbers(h)
+    iota(v("ONE"), [[0, 128]], 1, 0)
+    iota(v("GB", 64, 128), [[1, 8], [0, 8]], 0, 0)
+    asel(v("RNB"), v("ONE", 0, 64), [[4, 4], [16, 8], [0, 2]], 0, -1)
+    ts(pc(10), pc(1), 5.0, LT)
+    ts(pc(13), pc(5), 2.0, MUL, pc(6), ADD)
+    ts(v("A03"), row, pc(0), EQ, pc(10), MUL)
+    ts(v("W4"), row, pc(11), EQ, 1.0 / 16, MUL)
+    ts(v("W5"), row, pc(12), EQ)
+    tt(v("W5N"), v("W4"), v("W5"), SUB)
+    ts(v("SGL"), v("ROW", 0, 64), 16.0, MUL, pc(13), ADD)
+    cp(v("SNL"), v("SNI"))
+    cp(v("S1", 0, 512), ind(own("PHI"), v("SNL")))
+    act(v("SBR"), ind(own("RR"), v("SNL")))
+    lin(v("WA", 0, 64), v("GB", 64, 128), pc(15), pc(37))
+    lin(v("WA", 128, 160), v("GB", 64, 96), pc(38), pc(36))
+    for h in range(8, 12):
+        numbers(h)
+    send("a0", v("S1", 0, 512), "PHI")
+    ts(ghost("HI"), v("S1", 0, 512), ROUND16, ADD, -ROUND16, ADD)
+    mms(v("pX"), [(v("A03"), v("SBR")), (v("W5"), v("S1", 0, 512)), (v("W5N"), ghost("HI"))])
+    act(v("S1", 512, 1024), v("pX"))
+    iota(v("MKI"), [[0, 32], [1, 2], [0, 8]], 0, 0)
+    send("b0", v("S1", 512, 1024), "SC1")
+    asel(v("R2T"), v("ONE", 0, 64), [[-2, 64]], 0, 1, GE)
+    asel(v("R2"), v("R2T"), [[2, 64]], 1, -1, GE)
+    asel(v("RU"), v("ONE", 0, 32), [[4, 2], [8, 2], [16, 8]], 0, -1)
+
+    def neighbours_a(lst):
+        cp(v("NBS"), ind(v("NBI"), v(lst)))
+        for b in range(8):
+            mm(v("pC", b, 512, 8), v("NBS", b, 1024, 8), v("RNB"))
+
+    def neighbours_b(dst, between):
+        tt(v("LM"), v("pC"), v("MK"), MUL)
+        for k in range(4):
+            mm(part("pW", 64, k), part("LM", 128, k), v("R2"))
+        between()
+        for b in range(8):
+            mm(v("pU", b, 256, 8), v("NBS", b, 1024, 8), v("RU"))
+        return lambda: cp(v(dst), v("pW", 0, 256))
+
+    def blocks(a, b, dst):
+        asel(v("WT", a, b), v("WA", a, b), [[0, (b - a) // 8], [-16, 8]], 0, 1, GE)
+        asel(dst, v("WT", a, b), [[0, (b - a) // 8], [16, 8]], 15, -1, GE)
+
+    def own_pieces(h):
+        mms(v("pY%d" % h), [(v("A03"), part("RR", 512, h)), (v("W5"), part("PHI", 512, h)), (v("W5N"), part("HI", 512, h))])
+        act(part("SC1", 512, h), v("pY%d" % h))
+
+    neighbours_a("SGL")
+    iota(v("WA", 160, 176), [[-24576, 2], [0, 8]], 16384, 0)
+    blocks(0, 64, v("WB", 0, 64))
+    blocks(128, 176, v("WB", 128, 176))
+    act(v("PSG"), ind(own("PHI"), v("SGL")))
+    ts(v("MK"), v("MKI"), pc(3), EQ)
+    ts(own("HI"), own("PHI"), ROUND16, ADD, -ROUND16, ADD)
+    own_pieces(0)
+    fin = neighbours_b("NL1", lambda: own_pieces(1))
+    ts(pc(18), pc(0), -64.0, MUL, 1.0 - rank, ADD)
+    ts(pc(22), pc(0), 8.0, MUL)
+    ts(pc(19), pc(3), 56.0, MUL, pc(18), ADD)
+    fin()
+    iota(v("GB", 0, 64), [[0, 8], [2, 8]], 0, 0)
+    asel(v("R2A"), v("ONE", 0, 64), [[-2, 64]], 0, 1)
+    asel(v("R2B"), v("ONE", 0, 64), [[-2, 64]], -1, 1)
+    for nm in ("LA", "LB", "LE", "LH"):
+        iota(v(nm), [[0, 128]], 0, 0)
+    iota(ghost("OT"), [[0, 512]], 192, 0)
+    iota(ghost("O2"), [[0, 512]], 0, 0)
+    asel(v("IDB"), v("ONE"), [[-1, 128]], 0, 1)
+    iota(own("WK2"), [[0, 1024]], 0, 0)
+    iota(v("WA", 184, 192), [[0, 8]], 512, 0)
+    blocks(184, 192, v("WM2"))
+    col, loc = [[0, 8], [1, 16]], [[0, 8], [-1, 16]]
+    asel(v("A45"), v("IDB"), col, -5, 0, GE)
+    asel(v("A45"), v("A45"), loc, 6, 0, GE)
+    asel(v("A09"), v("IDB"), col, -5, 0, AL.not_equal)
+    asel(v("A09"), v("A09"), col, -6, 0, AL.not_equal)
+    asel(v("WQ"), v("ONE"), [[-16, 8], [-4, 16]], 28, 1, GE)
+    asel(v("WQ"), v("WQ"), [[16, 8], [4, 16]], -25, -1, GE)
+    asel(v("WQ"), v("WQ"), col, -7, 0, GE)
+    asel(v("WQ"), v("WQ"), loc, 10, 0, GE)
+    asel(v("PERM"), v("ONE"), [[-16, 8], [-1, 2], [-2, 8]], 0, 1)
+    wa = v("WA", 176, 184)
+    iota(wa, [[0, 8]], -256, 0)
+    asel(wa, wa, [[-16, 8]], -5, 1, AL.not_equal, -16.0)
+    asel(wa, wa, [[-16, 8]], -6, 1, AL.not_equal, -1.0)
+    asel(wa, wa, [[-16, 8]], -5, 1, GE)
+    asel(v("WB", 176, 184), wa, [[16, 8]], 10, -1, GE)
+    arrive("a0", "PHI")
+    arrive("b0", "SC1")
+    dma("S", ghost("PR"), ghost("RR"))
+    dma("S", ghost("P2R"), ghost("RR"))
+    dma("S", ghost("SCN"), ghost("SC1"))
+    dma("S", own("SC2"), own("SC1"))
+    dma("S", own("SC3"), own("SC1"))
+    dma("S", own("WK3"), own("WK2"))
+
+    SLOT = {0: 0, 2: 1, 1: 2}
+    CA, UA, THR, TT, JN, RT, CAJ, UAJ, T2, THS, DS, TS_, PQ, UD, SD, IY = [sm(k) for k in range(16)]
+    DU, PA, PB = v("pU", 256, 384), v("pU", 384, 448), v("pU", 448, 512)
+    XN, XN2 = v("XN", 0, 64), v("XN", 64, 128)
+    u3, c3, s3, pen3 = v("pU", 192, 256), v("pD", 0, 64), v("pX", 64, 128), v("PEN", 192, 256)
+
+    for rnd in range(3):
+        sc = "SC%d" % (rnd + 1)
+        wk = "WK%d" % (rnd + 1)
+        nl = "NL3" if rnd == 2 else "NL1"
+        mx = "M1" if rnd == 0 else "MM"
+        xw = v("PHI") if rnd == 0 else v("XT")
+        kw = v("SC1") if rnd == 0 else v("SCN")
+        mine = v(("PSG", "PS2", "YSG")[rnd])
+        w0 = 0 if rnd == 0 else 64
+        bias = pc(20) if rnd == 0 else pc(21)
+
+        def costs(k):
+            a = 1024 * k
+            cb, c0 = ("pD", 0) if k == 3 else ("pC", 64 * SLOT[k])
+            for b in range(8):
+                m, q = v(mx, a + b, a + 1024, 8), v("KG", a + b, a + 1024, 8)
+                if rnd == 0:
+                    pairs = [(v("PSG", b, 1024, 8), v("WB", 168, 176)), (m, v("WB", 160, 168)), (q, v("WB", 128 + 8 * k, 136 + 8 * k))]
+                    mms(v(cb, c0 + b, c0 + 64, 8), pairs if k < 3 else pairs[:2])
+                else:
+                    mm(v(cb, c0 + b, c0 + 64, 8), m, v("WM2"))
+
+        def big(k):
+            tt(part(mx, 1024, k), ind(xw, part(nl, 64, k)), mine, MAX)
+            if rnd > 0 or k == 3:
+                costs(k)
+
+        def small(k):
+            a = 1024 * k
+            act(part("KG", 1024, k), ind(kw, part(nl, 64, k)))
+            eb, e0, s0 = ("pX", 0, 64) if k == 3 else ("pE", 64 * SLOT[k], 192 + 64 * SLOT[k])
+            ws = v("WB", 152, 160) if rnd == 0 else v("WB", 176, 184)
+            for b in range(8):
+                mm(v(eb, e0 + b, e0 + 64, 8), v("KG", a + b, a + 1024, 8), v("WB", w0 + 8 * b, w0 + 8 * b + 8))
+            if rnd > 0 or k == 3:
+                for b in range(8):
+                    mm(v(eb, s0 + b, s0 + 64, 8), v("KG", a + b, a + 1024, 8), ws)
+            else:
+                costs(k)
+
+        for f, k in ((big, 0), (big, 1), (small, 0), (big, 2), (small, 1), (small, 2), (big, 3), (small, 3)):
+            f(k)
+        if rnd == 0:
+            ts(pc(20), pc(19), BIG1, MUL)
+            ts(pc(23), pc(3), -7.0, MUL, pc(22), ADD)
+            ts(XN, v("GB", 0, 64), pc(23), ADD)
+            ts(v("CP", 192, 256), v("GB", 0, 64), pc(23), ADD, DEF1, ADD)
+        ts(v("PEN", 0, 192), v("pE", 0, 192), bias, ADD, 0.0, MAX)
+        act(pen3, v("pX", 0, 64), AF.Relu, bias)
+        if rnd == 0:
+            mul(v("YT", 0, 1536), v("PHI"), 1.0 / 256)
+            lin(v("YP"), own("PHI"), 1.0 / 256, -LIFT)
+        if rnd == 1:
+            mul(v("YT", 1536, 2560), own("PHI"), 1.0 / 256)
+        if rnd == 2:
+            lin(v("YP"), ind(v("YT"), v("YL")), 1.0, -LIFT)
+
+        tt(v("PU", 0, 192), v("pU", 0, 192) if rnd == 0 else v("pE", 192, 384), v("PEN", 0, 192), ADD)
+        tt(v("CP", 0, 192), v("pC", 0, 192), v("PU", 0, 192), ADD)
+        ca, cb, ma, mb = v("CP", 0, 128), v("CP", 128, 256), v("M2", 0, 64), v("M2", 64, 128)
+        if rnd == 0:
+            tt(v("M2"), ca, cb, MIN)
+            tt(CA, ma, mb, MIN)
+            tt(PQ, s3, pen3, ADD)
+            cp(v("CI", 0, 64), CA)
+            tt(THR, CA, PQ, SUB)
+            ts(v("CI", 64, 128), v("CI", 0, 64), 2047, AND)
+            ua = v("CI", 64, 128)
+            tt(TT, c3, THR, LT)
+        else:
+            tt(v("T1"), cb, ca, LT)
+            tt(v("M2"), ca, cb, MIN)
+            tt(v("TD"), DU, v("T1"), MUL)
+            tt(T2, mb, ma, LT)
+            tt(v("U2"), v("pU", 0, 128), v("TD"), ADD)
+            tt(CA, ma, mb, MIN)
+            tt(PA, v("U2", 64, 128), v("U2", 0, 64), SUB)
+            if rnd == 1:
+                ts(CAJ, CA, BIG / 2, MIN)
+            tt(PB, PA, T2, MUL)
+            if rnd == 1:
+                ts(JN, CA, BIG / 2, GE)
+            tt(UA, PB, v("U2", 0, 64), ADD)
+            tt(PQ, s3, pen3, ADD)
+            if rnd == 1:
+                tt(PA, XN, UA, SUB)
+            tt(THR, CAJ if rnd == 1 else CA, PQ, SUB)
+            ua = UA
+            if rnd == 1:
+                tt(PB, PA, JN, MUL)
+            tt(TT, c3, THR, LT)
+            if rnd == 1:
+                tt(UAJ, PB, UA, ADD)
+                ua = UAJ
+        tt(PA, u3, ua, SUB)
+        tt(PB, PA, TT, MUL)
+        tt(v("LA", 0, 128, 2), PB, ua, ADD)
+        tt(v("LB", 1, 128, 2), PB, ua, ADD)
+        t_to_list("LA", "LB", 256)
+        if rnd == 0:
+            ts(pc(24), pc(2), 16.0, MUL, 15.0, ADD)
+            ts(pc(25), oh(0), 128.0, MUL, oh(1), ADD)
+            ts(v("Z"), v("ROW"), pc(24), EQ, pc(25), MUL)
+        if rnd == 1:
+            tt(THS, CA, PQ, SUB)
+            tt(DS, u3, UA, SUB)
+            tt(RT, JN, TT, AL.is_gt)
+        cp(v("UL"), v("pW", 256, 320))
+
+        tt(own("OT"), ind(v("YT", 0, 1536), v("UL")), v("YP"), SUB)
+        act(own("PR"), ind(v("RR"), v("UL")))
+        if rnd == 1:
+            lin(v("OB"), own("OT"), 1.0, -384.0)
+        else:
+            ts(v("OB"), own("OT"), -384.0, ADD)
+        if rnd == 0:
+            pl = "UL"
+        else:
+            pl = "PL"
+            fin = to_list("PR", 64, "PL", 0)
+            if rnd == 1:
+                tt(TS_, c3, THS, LT)
+                tt(PA, TS_, DS, MUL)
+                tt(UD, PA, UA, ADD)
+                tt(PA, UD, XN2, SUB)
+            fin()
+        tt(own("O2"), ind(v("OT"), v(pl)), v("OB"), ADD)
+        act(own("P2R"), ind(v("PR"), v(pl)))
+        fin = to_list("P2R", 64, "P2L", 64)
+        if rnd < 2:
+            dma("S", v("O2B"), own("O2"))
+            act(v("P2S"), ind(own("P2R"), v("SNL")))
+        if rnd == 1:
+            cp(v("O2S"), ind(own("O2"), v("SNL")))
+        fin()
+        if rnd < 2:
+            fin = to_list("P2S", 32, "QL", 128)
+        if rnd == 0:
+            ht = "O2"
+            cp(v("SCN", 0, 512), ind(v(sc), v("P2L", 0, 32)))
+            act(v("SCN", 512, 1024), ind(v(sc), v("P2L", 32, 64)))
+            cp(v("O2S"), ind(own("O2"), v("SNL")))
+            mul(v("PS2"), v("PSG"), 1.0 / 256)
+        else:
+            ht = "HT"
+            tt(own("HT"), ind(v(wk), v("P2L")), own("O2"), ADD)
+            act(own("SCN"), ind(v(sc), v("P2L")))
+
+        if rnd == 2:
+            top = (0, 8, 1)
+            for h in range(2):
+                act(part("BF", 512, h), ind(v("SCN"), part("P2L", 32, h)))
+                mm(v("pY%d" % h, rows=top), v("WB", 64, 72), part("BF", 512, h))
+            for h in range(4):
+                tt(part("YK", 256, h), ind(v("HT"), part("P2L", 16, h)), part("O2", 256, h), ADD)
+                dma("S", hbm(T.yk[:, 256 * h:256 * h + 256]), part("YK", 256, h))
+            ts(v("YR", 0, 512, rows=top), v("pY0", rows=top), 1.0 / BIG, MUL)
+            mul(v("YR", 512, 1024, rows=top), v("pY1", rows=top), 1.0 / BIG)
+            dma("A", hbm(T.yr[:]), v("YR", rows=top))
+            break
+
+        so = "S%d" % (rnd + 2)
+        nsc, nwk = "SC%d" % (rnd + 2), "WK%d" % (rnd + 2)
+        fin()
+        tt(v(so, 0, 512), ind(v(ht), v("QL")), v("O2S"), ADD)
+        act(v("SBR"), ind(v("SCN"), v("QL")))
+        send("a%d" % (rnd + 1), v(so, 0, 512), nwk)
+        mms(v("pX"), [(v("A45"), v("S1", 512, 1024)), (v("WQ"), v(so, 0, 512)), (v("A03"), v("SBR"))])
+        act(v(so, 512, 1024), v("pX"))
+        send("b%d" % (rnd + 1), v(so, 512, 1024), nsc)
+
+        if rnd == 1:
+            tt(PB, PA, RT, MUL)
+            tt(v("LE", 0, 128, 2), PB, XN2, ADD)
+            tt(v("LH", 1, 128, 2), PB, XN2, ADD)
+            t_to_list("LE", "LH", 320)
+            ts(IY, RT, 1536.0, MUL, -1536.0, ADD)
+            ts(v("CP", 192, 256), RT, 0.75 * BIG, MUL, -0.25 * BIG, ADD)
+            tt(SD, v("LE", 0, 128, 2), IY, ADD)
+            ts(v("WN"), v("pW", 320, 384), 1023.0, MIN)
+            cp(v("YL"), v("pW", 320, 384))
+            mm(v("pW", 384, 448), v("PERM"), v("WN"))
+        else:
+            ts(v("IDS"), v("IDB"), 1.0 / 256, MUL)
+        act(own("RR"), ind(v("P2R"), v("P2L")))
+        tt(v("KB"), ind(v("O2"), v("P2L")), v("O2B"), ADD)
+        if rnd == 1:
+            cp(v("SL"), v("pW", 384, 448))
+        for h in range(2):
+            mms(v("pY%d" % h), [(v("IDS"), part("PHI", 512, h)), (v("IDB"), part("KB", 512, h))])
+        arrive("a%d" % (rnd + 1), nwk)
+        mms(v("pX"), [(v("IDS"), ghost("PHI")), (v("IDB"), ghost(nwk))])
+        if rnd == 0:
+            ts(JN, CA, DEF1, GE)
+            cp(IY, v("pU", 0, 64))
+            tt(v("pU", 320, 384), XN, v("pU", 64, 128), SUB)
+            tt(RT, JN, TT, AL.is_gt)
+            tt(v("pU", 256, 320), v("pU", 128, 192), IY, SUB)
+            ts(v("CP", 192, 256), RT, 1.75 * BIG, MUL, -0.25 * BIG, ADD)
+        for h in range(2):
+            (cp if rnd == 0 else act)(part("YT", 512, h), v("pY%d" % h))
+        act(ghost("XT"), v("pX"))
+        if rnd == 0:
+            mul(v("WB", 64, 128), v("WB", 0, 64), BIG / BIG1)
+            mul(pc(21), pc(19), BIG)
+            lin(XN2, XN, 1.0, 1536.0)
+        fin = to_list("RR", 64, "RL", 448)
+        if rnd == 1:
+            neighbours_a("SL")
+        for h in range(2):
+            mms(v("pY%d" % h), [(v("A45"), part("SC1", 512, h)), (v("WQ"), part("KB", 512, h))], True, False)
+        fin()
+
+        arrive("b%d" % (rnd + 1), nsc)
+        dma("S", ghost("SCN"), ghost(nsc))
+        dma("S", ghost("HT"), ghost(nwk))
+        if rnd == 1:
+            act(v("YSG"), ind(own("YT"), v("SL")))
+            fin = neighbours_b("NL3", lambda: None)
+        tt(own("XT"), ind(v(nwk), v("RL")), own("YT"), ADD)
+        if rnd == 1:
+            fin()
+            cp(IY, v("pU", 0, 64))
+            tt(v("pU", 320, 384), SD, v("pU", 64, 128), SUB)
+            tt(v("pU", 256, 320), v("pU", 128, 192), IY, SUB)
+        for h in range(2):
+            act(part("TMP", 512, h), ind(v(nsc), part("RL", 32, h)))
+            mm(v("pY%d" % h), v("A09"), part("TMP", 512, h), False, True)
+        for h in range(2):
+            act(part("SCN", 512, h), v("pY%d" % h))
+
+    _emit(g, T, ops)

@@ -3,34 +3,32 @@ from concourse.mybir import AluOpType, ActivationFunctionType
 F, H16, I32, U16, F16 = "float32", "bfloat16", "int32", "uint16", "float16"
 SCRATCH = {}
 for _d, _l in (
-    (U16, "SNL 32 SGL 64 NL1 256 NL3 256 UL 64 PL 64 P2L 64 RL 64 QL 32 SL 64 YL 64"),
-    (I32, "SNI 32 NBI 1024 PI 16 CI 128"),
-    (F16, "NBS 1024 LM 512"),
-    (H16, "PHI 1536 PSG 1024 PS2 1024 HI 1536 SC1 1536 SC2 1536 SC3 1536 SCN 1536 TMP 1024 WK2 1536 WK3 1536 RR 1536 "
-          "PR 1536 P2R 1536 OT 1536 OB 1024 O2 1536 O2B 1024 HT 1536 KB 1024 SBR 512 O2S 512 P2S 512 S1 1024 S2 1024 "
-          "S3 1024 M1 4096 KG 4096 BF 1024"),
-    (F, "YP 1024 YSG 1024 YT 2560 XT 1536 MM 4096 YK 1024 YR 1024"),
-    (H16, "MKI 512 MK 512 RNB 64 RU 32 R2 64 IDB 128 IDS 128 Z 144 W4 128 W5 128 W5N 128 A03 128 A45 128 A09 128 "
-          "WQ 128 WB 192"),
-    (F, "PC 48 ROW 144 GB 128 OH 16 STB 12 ONE 128 R2T 64 R2A 64 R2B 64 PERM 128 WA 192 WT 192 WM2 8 XN 128"),
-    (F, "PEN 256 PU 256 CP 256 T1 128 M2 128 TD 128 U2 128 SM 1024 LA 128 LB 128 LE 128 LH 128 WN 64"),
+    (U16, "SNL 32 NL1 256 NL3 256 UL 64 PL 64 P2L 64 RL 64 YL 64 GL 8 GY 8"),
+    (I32, "SNI 32 NBQ 256 NBI 2048 PI 16"),
+    (F16, "NBH 256 NBS 1024 LM 512 LH 128 LY 128 M2 4096"),
+    (H16, "PHI 1536 PH2 1024 HI 1024 HS 512 NUM 1536 SC1 1536 SC2 1536 SC3 1536 TB2 1536 TB3 1536 ST 1024 DG 1024 "
+          "WK2 1536 WK3 1536 RR 1024 PR 1536 P2R 1536 OT 1536 OB 1024 O2 1536 O2B 1024 KB 1024 SBR 512 S1 1024 "
+          "S2 1536 S3 1536 M1 4096 KG 4096 BF 1024 PEN 256 DEFT 320"),
+    (F, "YP 1024 XS 1024 XT 2560 M3 4096 YK 1024 YR 64 KEEP 320 RM 320 ZZ 320 RESET 320 YY 64 SS 64"),
+    (H16, "MK 128 RNB 256 RD 160 R2 64 IDB 128 Z 144 ZB 144 W4 128 W5 128 W5N 128 A67 128 WQ0 128 "
+          "WM 8 WS 8 WE 64"),
+    (F, "PC 48 ROW 144 GB 192 OH 16 STB 12 ONE 160 RDT 160 RDU 160 MKI 128 WA 128 WMF 8 XN 64"),
 ):
     _w = _l.split()
     for _k in range(0, len(_w), 2):
         SCRATCH[_w[_k]] = ("sbuf", [128, int(_w[_k + 1])], _d)
-for _n in ("pC", "pD", "pE", "pU", "pX", "pY0", "pY1", "pW"):
+for _n in ("pK", "pD", "pE0", "pE1", "pW", "pX", "pY0", "pY1"):
     SCRATCH[_n] = ("psum", [128, 512], F)
-SEMAPHORES = ["cV", "cA", "cP", "cG", "sent", "a0", "a1", "a2", "b0", "b1", "b2"] + ["d%d" % k for k in range(24)]
+SEMAPHORES = ["cV", "cA", "cP", "cG", "sent", "a0", "a1", "a2", "b0", "b1", "b2", "c1", "c2"] + ["d%d" % k for k in range(30)]
 
 AL = AluOpType
 AF = ActivationFunctionType
 ADD, SUB, MUL, MAX, MIN, LT, GE, EQ = AL.add, AL.subtract, AL.mult, AL.max, AL.min, AL.is_lt, AL.is_ge, AL.is_equal
 BIG = float(2 ** 22)
-BIG1 = float(2 ** 26)
-MID1 = 2040.0 * 8192.0
-DEF1 = 16719872.0
-LIFT = 192.0 + 1.0 / 512
+HUGE = 1e12
+LIFT = 49152.0
 ROUND16 = 1.5 * 2 ** 27
+VH = (384, 256, 256)
 
 
 def _emit(g, T, ops):
@@ -119,9 +117,6 @@ def rank_program(g, core, T, topo):
     def part(name, n, h):
         return v(name, n * h, n * h + n)
 
-    def sm(k):
-        return part("SM", 64, k)
-
     def pc(k):
         return part("PC", 1, k)
 
@@ -148,6 +143,9 @@ def rank_program(g, core, T, topo):
             rec("V", lambda: g.vector.tensor_scalar(out[0], a[0], val(s1), None, op0), [out], [a] + aps(s1))
         else:
             rec("V", lambda: g.vector.tensor_scalar(out[0], a[0], val(s1), val(s2), op0, op1), [out], [a] + aps(s1, s2))
+
+    def scan(out, a, b, op0, op1):
+        rec("V", lambda: g.vector.tensor_tensor_scan(out[0], a[0], b[0], 0.0, op0, op1), [out], [a, b])
 
     def ms(out, c):
         rec("V", lambda: g.vector.memset(out[0], c), [out], [])
@@ -197,13 +195,10 @@ def rank_program(g, core, T, topo):
     def arrive(sem, dst):
         rec("X", None, [v(dst, 1024, 1536)], [], own=(sem, len(topo.engines(prv, core))))
 
-    def to_list(src, n, dst, col):
+    def to_list(src, dst, col):
         for i in range(16):
-            mm(v("pW", col, col + n), v("Z", 15 - i, 143 - i), v(src, i, 16 * n, 16), i == 0, i == 15)
-        return lambda: cp(v(dst, 0, n), v("pW", col, col + n))
-
-    def t_to_list(la, lb, col):
-        mms(v("pW", col, col + 64), [(v(la), v("R2A")), (v(lb), v("R2B"))])
+            mm(v("pW", col, col + 64), v("Z", 15 - i, 143 - i), v(src, i, 1024, 16), i == 0, i == 15)
+        return lambda: cp(v(dst), v("pW", col, col + 64))
 
     def own(name):
         return v(name, 0, 1024)
@@ -211,377 +206,336 @@ def rank_program(g, core, T, topo):
     def ghost(name):
         return v(name, 1024, 1536)
 
-    row = v("ROW", 0, 128)
+    def at(name, pos):
+        return v(name, pos, 320, 5)
 
-    def numbers(h):
-        lin(part("RR", 128, h), row, oh(1), part("STB", 1, h))
+    row = v("ROW", 0, 128)
+    IDB = v("IDB")
 
     AND, SHR = AL.bitwise_and, AL.logical_shift_right
     p = v("PI", 0, 1)
-    dma("A", own("PHI"), hbm(T.phi[:]))
     dma("S", v("SNI"), hbm(T.snd[:]))
+    dma("A", own("PHI"), hbm(T.phi[:]))
+    dma("S", v("NBQ"), hbm(T.nb[:]))
     iota(p, [[0, 1]], 0, 1, False)
     iota(v("ROW"), [[1, 144]], 0, 0)
-    iota(v("NBI", 512, 1024), [[0, 512]], 0, 0, False)
-    ms(v("NBI", 0, 256), 0)
+    ms(v("ONE"), 1.0)
+    ms(v("DEFT"), 0.0)
     ts(v("PI", 1, 2), p, 15, AND)
     ts(v("PI", 2, 3), p, 4, SHR)
     ts(v("PI", 3, 4), p, 1, AND)
-    cp(v("PC", 0, 4), v("PI", 0, 4))
-    ms(v("NBI", 256, 512), 0)
-    dma("S", v("NBI", rows=(0, 128, 4)), hbm(T.nb[:]))
-    ts(v("OH"), v("ROW", 0, 16), pc(1), EQ)
-    ts(v("PI", 5, 6), p, 7, AND)
-    ts(pc(4), oh(3), float(rank), MUL, oh(2), ADD)
-    ts(v("PI", 6, 7), p, 3, SHR, 1, AND)
-    ts(pc(9), pc(4), oh(4), ADD)
-    cp(v("PC", 5, 7), v("PI", 5, 7))
-    ts(v("STB"), v("ROW", 0, 12), oh(0), MUL, pc(9), ADD)
-    lin(pc(11), pc(2), 16.0, 5.0)
-    lin(pc(12), pc(2), 16.0, 6.0)
-    lin(pc(14), oh(0), 1024.0, oh(3))
-    lin(pc(16), oh(5), 16.0, oh(6))
-    mul(pc(35), oh(2), -MID1)
-    lin(pc(17), oh(1), 8.0, pc(14))
-    lin(pc(36), pc(16), -8192.0, pc(35))
-    mul(pc(15), oh(2), -16.0 * BIG1)
-    mul(pc(37), pc(17), BIG1)
-    mul(pc(38), oh(4), 2048.0)
-    for h in range(8):
-        numbers(h)
-    iota(v("ONE"), [[0, 128]], 1, 0)
+    ts(v("PI", 4, 5), p, 7, AND)
+    ts(v("PI", 5, 6), p, 3, SHR, 1, AND)
+    ts(v("PI", 6, 7), p, 1, SHR)
+    cp(v("PC", 0, 7), v("PI", 0, 7))
+    iota(v("GB", 128, 192), [[4, 4], [16, 8], [0, 2]], 0, 0)
+    iota(v("MKI"), [[0, 8], [1, 2], [0, 8]], 0, 0)
+    iota(v("GB", 0, 64), [[0, 8], [1, 8]], 0, 0)
     iota(v("GB", 64, 128), [[1, 8], [0, 8]], 0, 0)
-    asel(v("RNB"), v("ONE", 0, 64), [[4, 4], [16, 8], [0, 2]], 0, -1)
-    ts(pc(10), pc(1), 5.0, LT)
-    ts(pc(13), pc(5), 2.0, MUL, pc(6), ADD)
-    ts(v("A03"), row, pc(0), EQ, pc(10), MUL)
+    ts(v("OH"), v("ROW", 0, 16), pc(1), EQ)
+    ts(pc(11), pc(2), 16.0, MUL, 6.0, ADD)
+    ts(pc(9), oh(4), float(rank), MUL, oh(5), ADD)
+    ts(pc(7), oh(0), oh(2), ADD)
+    ts(pc(8), oh(1), oh(3), ADD)
+    ts(v("STB", 0, 8), v("ROW", 0, 8), pc(7), MUL, pc(9), ADD)
+    for h in range(8):
+        lin(part("NUM", 128, h), row, pc(8), part("STB", 1, h))
+    for q in range(4):
+        ts(part("RNB", 64, q), v("GB", 128, 192), float(q), ADD, pc(0), EQ)
+    ts(v("STB", 8, 12), v("ROW", 8, 12), oh(0), MUL)
+    ts(pc(10), pc(1), 2.0, GE)
     ts(v("W4"), row, pc(11), EQ, 1.0 / 16, MUL)
-    ts(v("W5"), row, pc(12), EQ)
-    tt(v("W5N"), v("W4"), v("W5"), SUB)
-    ts(v("SGL"), v("ROW", 0, 64), 16.0, MUL, pc(13), ADD)
+    ts(v("W5"), row, -1.0, ADD, pc(11), EQ)
+    ts(pc(12), pc(1), 5.0, AL.is_le, pc(10), MUL)
+    asel(IDB, v("ONE", 0, 128), [[-1, 128]], 0, 1)
     cp(v("SNL"), v("SNI"))
+    dma("S", v("PH2"), own("PHI"))
+    tt(v("W5N"), v("W4"), v("W5"), SUB)
+    cp(v("NBH"), v("NBQ"))
     cp(v("S1", 0, 512), ind(own("PHI"), v("SNL")))
-    act(v("SBR"), ind(own("RR"), v("SNL")))
-    lin(v("WA", 0, 64), v("GB", 64, 128), pc(15), pc(37))
-    lin(v("WA", 128, 160), v("GB", 64, 96), pc(38), pc(36))
+    mul(v("SBR"), ind(own("NUM"), v("SNL")), pc(12))
     for h in range(8, 12):
-        numbers(h)
+        lin(part("NUM", 128, h), row, oh(1), part("STB", 1, h))
     send("a0", v("S1", 0, 512), "PHI")
-    ts(ghost("HI"), v("S1", 0, 512), ROUND16, ADD, -ROUND16, ADD)
-    mms(v("pX"), [(v("A03"), v("SBR")), (v("W5"), v("S1", 0, 512)), (v("W5N"), ghost("HI"))])
-    act(v("S1", 512, 1024), v("pX"))
-    iota(v("MKI"), [[0, 32], [1, 2], [0, 8]], 0, 0)
-    send("b0", v("S1", 512, 1024), "SC1")
-    asel(v("R2T"), v("ONE", 0, 64), [[-2, 64]], 0, 1, GE)
-    asel(v("R2"), v("R2T"), [[2, 64]], 1, -1, GE)
-    asel(v("RU"), v("ONE", 0, 32), [[4, 2], [8, 2], [16, 8]], 0, -1)
-
-    def neighbours_a(lst):
-        cp(v("NBS"), ind(v("NBI"), v(lst)))
+    ts(v("HS"), v("S1", 0, 512), ROUND16, ADD, -ROUND16, ADD)
+    for q in range(4):
         for b in range(8):
-            mm(v("pC", b, 512, 8), v("NBS", b, 1024, 8), v("RNB"))
+            mm(v("pY1", b, 512, 8, rows=(32 * q, 32 * q + 32, 1)), v("NBH", b, 256, 8), part("RNB", 64, q))
+    mms(v("pX"), [(v("W5"), v("S1", 0, 512)), (IDB, v("SBR")), (v("W5N"), v("HS")), (IDB, ghost("NUM"))])
+    act(v("S1", 512, 1024), v("pX"))
+    send("b0", v("S1", 512, 1024), "SC1")
+    ts(v("MK"), v("MKI"), pc(3), EQ)
+    ts(v("HI"), own("PHI"), ROUND16, ADD, -ROUND16, ADD)
+    ts(v("R2"), v("ROW", 0, 64), pc(6), EQ)
 
-    def neighbours_b(dst, between):
-        tt(v("LM"), v("pC"), v("MK"), MUL)
+    def masked(bank, ks):
+        for k in ks:
+            tt(part("LM", 128, k), part(bank, 128, k), v("MK"), MUL)
+
+    def nb_lists(dst):
         for k in range(4):
             mm(part("pW", 64, k), part("LM", 128, k), v("R2"))
-        between()
-        for b in range(8):
-            mm(v("pU", b, 256, 8), v("NBS", b, 1024, 8), v("RU"))
         return lambda: cp(v(dst), v("pW", 0, 256))
 
-    def blocks(a, b, dst):
-        asel(v("WT", a, b), v("WA", a, b), [[0, (b - a) // 8], [-16, 8]], 0, 1, GE)
-        asel(dst, v("WT", a, b), [[0, (b - a) // 8], [16, 8]], 15, -1, GE)
+    def own_pieces(h, bank):
+        mms(v(bank), [(IDB, part("NUM", 512, h)), (v("W5"), part("PHI", 512, h)), (v("W5N"), part("HI", 512, h))])
+        act(part("SC1", 512, h), v(bank))
 
-    def own_pieces(h):
-        mms(v("pY%d" % h), [(v("A03"), part("RR", 512, h)), (v("W5"), part("PHI", 512, h)), (v("W5N"), part("HI", 512, h))])
-        act(part("SC1", 512, h), v("pY%d" % h))
-
-    neighbours_a("SGL")
-    iota(v("WA", 160, 176), [[-24576, 2], [0, 8]], 16384, 0)
-    blocks(0, 64, v("WB", 0, 64))
-    blocks(128, 176, v("WB", 128, 176))
-    act(v("PSG"), ind(own("PHI"), v("SGL")))
-    ts(v("MK"), v("MKI"), pc(3), EQ)
-    ts(own("HI"), own("PHI"), ROUND16, ADD, -ROUND16, ADD)
-    own_pieces(0)
-    fin = neighbours_b("NL1", lambda: own_pieces(1))
-    ts(pc(18), pc(0), -64.0, MUL, 1.0 - rank, ADD)
-    ts(pc(22), pc(0), 8.0, MUL)
-    ts(pc(19), pc(3), 56.0, MUL, pc(18), ADD)
+    own_pieces(0, "pY0")
+    masked("pY1", range(4))
+    fin = nb_lists("NL1")
+    own_pieces(1, "pE0")
+    ts(pc(13), oh(6), -16.0, MUL, oh(7), SUB)
+    ts(pc(14), oh(8), oh(9), ADD)
+    ts(pc(15), oh(2), 1024.0, MUL, oh(4), ADD)
+    ts(pc(16), oh(5), 16384.0, MUL, pc(13), ADD)
+    ts(pc(17), oh(3), 8.0, MUL, pc(15), ADD)
     fin()
-    iota(v("GB", 0, 64), [[0, 8], [2, 8]], 0, 0)
-    asel(v("R2A"), v("ONE", 0, 64), [[-2, 64]], 0, 1)
-    asel(v("R2B"), v("ONE", 0, 64), [[-2, 64]], -1, 1)
-    for nm in ("LA", "LB", "LE", "LH"):
-        iota(v(nm), [[0, 128]], 0, 0)
-    iota(ghost("OT"), [[0, 512]], 192, 0)
-    iota(ghost("O2"), [[0, 512]], 0, 0)
-    asel(v("IDB"), v("ONE"), [[-1, 128]], 0, 1)
-    iota(own("WK2"), [[0, 1024]], 0, 0)
-    iota(v("WA", 184, 192), [[0, 8]], 512, 0)
-    blocks(184, 192, v("WM2"))
+    ts(v("WM"), v("ROW", 0, 8), pc(2), EQ, 2.0, MUL)
+    ms(at("DEFT", 4), BIG / 2)
+    pat = [[-1, 4], [-16, 8], [4, 5]]
+    asel(v("RDT"), v("ONE"), pat, -12, 1)
+    asel(v("RDU"), v("RDT"), pat, -8, 1, AL.not_equal, -1.0)
+    asel(v("RD"), v("RDU"), [[-1, 4], [-16, 8], [0, 5]], 0, 1, GE)
+    iota(v("XN"), [[1, 8], [0, 8]], 0, 8)
+    iota(v("RESET"), [[0, 320]], 0, 0)
+    iota(ghost("OT"), [[0, 512]], int(LIFT), 0)
     col, loc = [[0, 8], [1, 16]], [[0, 8], [-1, 16]]
-    asel(v("A45"), v("IDB"), col, -5, 0, GE)
-    asel(v("A45"), v("A45"), loc, 6, 0, GE)
-    asel(v("A09"), v("IDB"), col, -5, 0, AL.not_equal)
-    asel(v("A09"), v("A09"), col, -6, 0, AL.not_equal)
-    asel(v("WQ"), v("ONE"), [[-16, 8], [-4, 16]], 28, 1, GE)
-    asel(v("WQ"), v("WQ"), [[16, 8], [4, 16]], -25, -1, GE)
-    asel(v("WQ"), v("WQ"), col, -7, 0, GE)
-    asel(v("WQ"), v("WQ"), loc, 10, 0, GE)
-    asel(v("PERM"), v("ONE"), [[-16, 8], [-1, 2], [-2, 8]], 0, 1)
-    wa = v("WA", 176, 184)
-    iota(wa, [[0, 8]], -256, 0)
-    asel(wa, wa, [[-16, 8]], -5, 1, AL.not_equal, -16.0)
-    asel(wa, wa, [[-16, 8]], -6, 1, AL.not_equal, -1.0)
-    asel(wa, wa, [[-16, 8]], -5, 1, GE)
-    asel(v("WB", 176, 184), wa, [[16, 8]], 10, -1, GE)
+    asel(at("RESET", 0), at("RESET", 1), [[0, 64]], 0, 0, AL.not_equal, HUGE)
+    asel(v("A67"), IDB, col, -6, 0, GE)
+    asel(v("A67"), v("A67"), loc, 7, 0, GE)
+    iota(ghost("O2"), [[0, 512]], 0, 0)
+    iota(own("WK2"), [[0, 1024]], 0, 0)
+    iota(v("NBI", 0, 1024), [[0, 1024]], 0, 0, False)
+    iota(v("NBI", 1024, 2048), [[0, 1024]], 0, 0, False)
     arrive("a0", "PHI")
     arrive("b0", "SC1")
-    dma("S", ghost("PR"), ghost("RR"))
-    dma("S", ghost("P2R"), ghost("RR"))
-    dma("S", ghost("SCN"), ghost("SC1"))
-    dma("S", own("SC2"), own("SC1"))
-    dma("S", own("SC3"), own("SC1"))
+    dma("S", ghost("PR"), ghost("SC1"))
+    dma("S", ghost("P2R"), ghost("SC1"))
+    dma("S", own("TB2"), own("NUM"))
+    dma("S", own("TB3"), own("NUM"))
     dma("S", own("WK3"), own("WK2"))
+    dma("S", v("NBI", 0, 1024, rows=(0, 128, 4)), hbm(T.nb[:]))
+    dma("S", v("NBI", 1024, 2048, rows=(0, 128, 4)), hbm(T.nb[:]))
 
-    SLOT = {0: 0, 2: 1, 1: 2}
-    CA, UA, THR, TT, JN, RT, CAJ, UAJ, T2, THS, DS, TS_, PQ, UD, SD, IY = [sm(k) for k in range(16)]
-    DU, PA, PB = v("pU", 256, 384), v("pU", 384, 448), v("pU", 448, 512)
-    XN, XN2 = v("XN", 0, 64), v("XN", 64, 128)
-    u3, c3, s3, pen3 = v("pU", 192, 256), v("pD", 0, 64), v("pX", 64, 128), v("PEN", 192, 256)
+    def default(u):
+        tt(at("pD", 3), at("pD", 3), u, SUB)
+        cp(at("pD", 4), u)
 
     for rnd in range(3):
-        sc = "SC%d" % (rnd + 1)
-        wk = "WK%d" % (rnd + 1)
         nl = "NL3" if rnd == 2 else "NL1"
-        mx = "M1" if rnd == 0 else "MM"
-        xw = v("PHI") if rnd == 0 else v("XT")
-        kw = v("SC1") if rnd == 0 else v("SCN")
-        mine = v(("PSG", "PS2", "YSG")[rnd])
-        w0 = 0 if rnd == 0 else 64
-        bias = pc(20) if rnd == 0 else pc(21)
+        mx = "M%d" % (rnd + 1)
+        xw = v("PHI") if rnd == 0 else v("XT", 1024, 2560)
+        kw = v("SC%d" % (rnd + 1))
+        mine = v("XS") if rnd == 2 else v("PH2")
+        wm = v("WMF") if rnd == 2 else v("WM")
+        unit = 256.0 if rnd == 2 else 1.0
 
-        def costs(k):
-            a = 1024 * k
-            cb, c0 = ("pD", 0) if k == 3 else ("pC", 64 * SLOT[k])
-            for b in range(8):
-                m, q = v(mx, a + b, a + 1024, 8), v("KG", a + b, a + 1024, 8)
-                if rnd == 0:
-                    pairs = [(v("PSG", b, 1024, 8), v("WB", 168, 176)), (m, v("WB", 160, 168)), (q, v("WB", 128 + 8 * k, 136 + 8 * k))]
-                    mms(v(cb, c0 + b, c0 + 64, 8), pairs if k < 3 else pairs[:2])
-                else:
-                    mm(v(cb, c0 + b, c0 + 64, 8), m, v("WM2"))
+        def key(k, b):
+            return v("pK", 40 * b + 3 - k, 40 * b + 40, 5)
 
         def big(k):
             tt(part(mx, 1024, k), ind(xw, part(nl, 64, k)), mine, MAX)
-            if rnd > 0 or k == 3:
-                costs(k)
 
-        def small(k):
-            a = 1024 * k
-            act(part("KG", 1024, k), ind(kw, part(nl, 64, k)))
-            eb, e0, s0 = ("pX", 0, 64) if k == 3 else ("pE", 64 * SLOT[k], 192 + 64 * SLOT[k])
-            ws = v("WB", 152, 160) if rnd == 0 else v("WB", 176, 184)
+        def big_mm(k):
             for b in range(8):
-                mm(v(eb, e0 + b, e0 + 64, 8), v("KG", a + b, a + 1024, 8), v("WB", w0 + 8 * b, w0 + 8 * b + 8))
-            if rnd > 0 or k == 3:
+                mm(key(k, b), v(mx, 1024 * k + b, 1024 * k + 1024, 8), wm, False, False)
+
+        def small(k, n=1024):
+            a = 1024 * k
+            act(v("KG", a, a + n), ind(kw, v(nl, 64 * k, 64 * k + n // 16)))
+
+        def small_mm(k):
+            a = 1024 * k
+            e0 = 64 * (k & 1)
+            for b in range(8):
+                mm(v("pE%d" % (k >> 1), e0 + 8 * b, e0 + 8 * b + 8), v("KG", a + b, a + 1024, 8), part("WE", 8, b))
+            for b in range(8):
+                mm(key(k, b), v("KG", a + b, a + 1024, 8), v("WS"), False, False)
+
+        def pen(j, stop=False):
+            act(part("PEN", 128, j), v("pE%d" % j, 0, 128), AF.Relu, pc(20))
+            return lambda: [mm(at("pK", 3 - k), IDB, part("PEN", 64, k), False, stop and k & 1 == 1) for k in (2 * j, 2 * j + 1)]
+
+        mm(v("pK", 0, 320), IDB, v("DEFT"), True, False)
+        vh = VH[rnd]
+        big(0)
+        if rnd == 0:
+            ts(pc(19), oh(5), -8.0, MUL)
+            ts(pc(18), pc(16), pc(14), SUB)
+            ts(v("WA", 64, 128), v("GB", 0, 64), pc(2), EQ, BIG, MUL)
+            ts(v("WA", 0, 64), v("GB", 64, 128), pc(19), MUL, pc(17), ADD)
+            ts(v("WS"), v("ROW", 0, 8), pc(2), EQ, pc(18), MUL)
+            ts(pc(20), pc(0), -64.0 * BIG, MUL, (1.0 - rank) * BIG, ADD)
+            tt(v("WE"), v("WA", 0, 64), v("WA", 64, 128), MUL)
+        small(0), big_mm(0), small_mm(0)
+        if rnd == 0:
+            for q in range(4):
                 for b in range(8):
-                    mm(v(eb, s0 + b, s0 + 64, 8), v("KG", a + b, a + 1024, 8), ws)
-            else:
-                costs(k)
-
-        for f, k in ((big, 0), (big, 1), (small, 0), (big, 2), (small, 1), (small, 2), (big, 3), (small, 3)):
-            f(k)
+                    mm(v("pD", 40 * b, 40 * b + 40, rows=(32 * q, 32 * q + 32, 1)), v("NBH", b, 256, 8), part("RD", 40, q))
+        big(1), small(1), big_mm(1), small_mm(1)
+        if vh:
+            cp(v("KG", 4096 - vh, 4096), ind(kw, v(nl, 256 - vh // 16, 256)))
+        big(2), small(2)
+        f0 = pen(0)
+        small_mm(2), big_mm(2)
+        f0()
+        big(3), small(3, 1024 - vh)
         if rnd == 0:
-            ts(pc(20), pc(19), BIG1, MUL)
-            ts(pc(23), pc(3), -7.0, MUL, pc(22), ADD)
-            ts(XN, v("GB", 0, 64), pc(23), ADD)
-            ts(v("CP", 192, 256), v("GB", 0, 64), pc(23), ADD, DEF1, ADD)
-        ts(v("PEN", 0, 192), v("pE", 0, 192), bias, ADD, 0.0, MAX)
-        act(pen3, v("pX", 0, 64), AF.Relu, bias)
-        if rnd == 0:
-            mul(v("YT", 0, 1536), v("PHI"), 1.0 / 256)
-            lin(v("YP"), own("PHI"), 1.0 / 256, -LIFT)
-        if rnd == 1:
-            mul(v("YT", 1536, 2560), own("PHI"), 1.0 / 256)
-        if rnd == 2:
-            lin(v("YP"), ind(v("YT"), v("YL")), 1.0, -LIFT)
-
-        tt(v("PU", 0, 192), v("pU", 0, 192) if rnd == 0 else v("pE", 192, 384), v("PEN", 0, 192), ADD)
-        tt(v("CP", 0, 192), v("pC", 0, 192), v("PU", 0, 192), ADD)
-        ca, cb, ma, mb = v("CP", 0, 128), v("CP", 128, 256), v("M2", 0, 64), v("M2", 64, 128)
-        if rnd == 0:
-            tt(v("M2"), ca, cb, MIN)
-            tt(CA, ma, mb, MIN)
-            tt(PQ, s3, pen3, ADD)
-            cp(v("CI", 0, 64), CA)
-            tt(THR, CA, PQ, SUB)
-            ts(v("CI", 64, 128), v("CI", 0, 64), 2047, AND)
-            ua = v("CI", 64, 128)
-            tt(TT, c3, THR, LT)
-        else:
-            tt(v("T1"), cb, ca, LT)
-            tt(v("M2"), ca, cb, MIN)
-            tt(v("TD"), DU, v("T1"), MUL)
-            tt(T2, mb, ma, LT)
-            tt(v("U2"), v("pU", 0, 128), v("TD"), ADD)
-            tt(CA, ma, mb, MIN)
-            tt(PA, v("U2", 64, 128), v("U2", 0, 64), SUB)
-            if rnd == 1:
-                ts(CAJ, CA, BIG / 2, MIN)
-            tt(PB, PA, T2, MUL)
-            if rnd == 1:
-                ts(JN, CA, BIG / 2, GE)
-            tt(UA, PB, v("U2", 0, 64), ADD)
-            tt(PQ, s3, pen3, ADD)
-            if rnd == 1:
-                tt(PA, XN, UA, SUB)
-            tt(THR, CAJ if rnd == 1 else CA, PQ, SUB)
-            ua = UA
-            if rnd == 1:
-                tt(PB, PA, JN, MUL)
-            tt(TT, c3, THR, LT)
-            if rnd == 1:
-                tt(UAJ, PB, UA, ADD)
-                ua = UAJ
-        tt(PA, u3, ua, SUB)
-        tt(PB, PA, TT, MUL)
-        tt(v("LA", 0, 128, 2), PB, ua, ADD)
-        tt(v("LB", 1, 128, 2), PB, ua, ADD)
-        t_to_list("LA", "LB", 256)
-        if rnd == 0:
+            ts(pc(21), pc(4), 40.0, MUL, 4.0, ADD)
+            default(v("XN"))
+            ts(v("GL"), v("ROW", 0, 8), 5.0, MUL, pc(21), ADD)
             ts(pc(24), pc(2), 16.0, MUL, 15.0, ADD)
             ts(pc(25), oh(0), 128.0, MUL, oh(1), ADD)
             ts(v("Z"), v("ROW"), pc(24), EQ, pc(25), MUL)
+        small_mm(3)
+        f0 = pen(1, True)
+        big_mm(3)
+        f0()
+        if rnd != 1:
+            lin(v("YP"), mine, 1.0, (-0.5 - LIFT) / unit)
+        else:
+            act(own("XT"), own("PHI"))
+
+        scan(v("RM"), v("RESET"), v("pK", 0, 320), MAX, MIN)
+        tt(v("KEEP"), v("pK", 0, 320), v("RM"), AL.not_equal)
+        scan(v("ZZ"), v("KEEP"), v("pD", 0, 320), MUL, ADD)
+        tt(v("LH"), ind(v("ZZ"), v("GL")), v("MK"), MUL)
+        mm(v("pW", 256, 320), v("LH"), v("R2"))
+        if rnd < 2:
+            ts(at("DEFT", 4), at("RM", 4), BIG / 2, GE, BIG / 2, MUL)
         if rnd == 1:
-            tt(THS, CA, PQ, SUB)
-            tt(DS, u3, UA, SUB)
-            tt(RT, JN, TT, AL.is_gt)
+            ts(v("pE0", 320, 384), at("RM", 3), 1.5 * BIG, LT, 2.0 / BIG, MUL)
         cp(v("UL"), v("pW", 256, 320))
 
-        tt(own("OT"), ind(v("YT", 0, 1536), v("UL")), v("YP"), SUB)
-        act(own("PR"), ind(v("RR"), v("UL")))
+        tt(own("OT"), ind(xw, v("UL")), v("YP"), SUB)
+        act(own("PR"), ind(kw, v("UL")))
         if rnd == 1:
-            lin(v("OB"), own("OT"), 1.0, -384.0)
+            lin(v("OB"), own("OT"), 1.0, -2 * LIFT)
         else:
-            ts(v("OB"), own("OT"), -384.0, ADD)
+            ts(v("OB"), own("OT"), -2 * LIFT / unit, ADD)
         if rnd == 0:
             pl = "UL"
         else:
             pl = "PL"
-            fin = to_list("PR", 64, "PL", 0)
+            fin = to_list("PR", "PL", 0)
             if rnd == 1:
-                tt(TS_, c3, THS, LT)
-                tt(PA, TS_, DS, MUL)
-                tt(UD, PA, UA, ADD)
-                tt(PA, UD, XN2, SUB)
+                e1, e2 = v("pE0", 384, 448), v("pE0", 448, 512)
+                tt(e1, v("pE0", 320, 384), at("DEFT", 4), MUL)
+                ts(v("YY"), at("DEFT", 4), 2048.0 / BIG, MUL)
+                tt(e2, e1, at("ZZ", 3), MUL)
+                tt(e1, e2, v("XN"), ADD)
+                tt(v("YY"), e1, v("YY"), ADD)
+                cp(v("SS"), e1)
+                tt(v("LY"), ind(v("YY"), v("GY")), v("MK"), MUL)
             fin()
-        tt(own("O2"), ind(v("OT"), v(pl)), v("OB"), ADD)
+            if rnd == 1:
+                mm(v("pW", 320, 384), v("LY"), v("R2"))
         act(own("P2R"), ind(v("PR"), v(pl)))
-        fin = to_list("P2R", 64, "P2L", 64)
-        if rnd < 2:
-            dma("S", v("O2B"), own("O2"))
-            act(v("P2S"), ind(own("P2R"), v("SNL")))
-        if rnd == 1:
-            cp(v("O2S"), ind(own("O2"), v("SNL")))
-        fin()
-        if rnd < 2:
-            fin = to_list("P2S", 32, "QL", 128)
         if rnd == 0:
-            ht = "O2"
-            cp(v("SCN", 0, 512), ind(v(sc), v("P2L", 0, 32)))
-            act(v("SCN", 512, 1024), ind(v(sc), v("P2L", 32, 64)))
-            cp(v("O2S"), ind(own("O2"), v("SNL")))
-            mul(v("PS2"), v("PSG"), 1.0 / 256)
+            for h in range(2):
+                tt(part("O2", 512, h), ind(v("OT"), part(pl, 32, h)), part("OB", 512, h), ADD)
+                (cp if h else act)(part("O2B", 512, h), part("O2", 512, h))
         else:
-            ht = "HT"
-            tt(own("HT"), ind(v(wk), v("P2L")), own("O2"), ADD)
-            act(own("SCN"), ind(v(sc), v("P2L")))
+            tt(own("O2"), ind(v("OT"), v(pl)), v("OB"), ADD)
+            if rnd == 1:
+                dma("S", v("O2B"), own("O2"))
+                cp(v("YL"), v("pW", 320, 384))
+            else:
+                cp(v("O2B"), own("O2"))
+        fin = to_list("P2R", "P2L", 64)
+        if rnd == 1:
+            mul(v("XS"), ind(v("XT", 0, 2048), v("YL")), 1.0 / 256)
+            cp(v("NBS"), ind(v("NBI"), v("YL")))
+        if rnd == 0:
+            ts(pc(29), pc(2), 16.0, MUL, pc(5), ADD)
+        fin()
+        if rnd == 0:
+            ts(v("WQ0"), row, -8.0, ADD, pc(29), EQ)
 
         if rnd == 2:
-            top = (0, 8, 1)
+            cuts = (0, 56, 64)
             for h in range(2):
-                act(part("BF", 512, h), ind(v("SCN"), part("P2L", 32, h)))
-                mm(v("pY%d" % h, rows=top), v("WB", 64, 72), part("BF", 512, h))
+                a, b = cuts[h], cuts[h + 1]
+                act(v("BF", 16 * a, 16 * b), ind(v("P2R"), v("P2L", a, b)))
+                for i in range(a // 4, b // 4):
+                    mm(v("pX", 0, 64), v("ZB", 15 - i, 143 - i), part("BF", 64, i), i == 0, i == 15)
             for h in range(4):
-                tt(part("YK", 256, h), ind(v("HT"), part("P2L", 16, h)), part("O2", 256, h), ADD)
+                tt(part("YK", 256, h), ind(v("O2"), part("P2L", 16, h)), part("O2B", 256, h), ADD)
                 dma("S", hbm(T.yk[:, 256 * h:256 * h + 256]), part("YK", 256, h))
-            ts(v("YR", 0, 512, rows=top), v("pY0", rows=top), 1.0 / BIG, MUL)
-            mul(v("YR", 512, 1024, rows=top), v("pY1", rows=top), 1.0 / BIG)
-            dma("A", hbm(T.yr[:]), v("YR", rows=top))
+            act(v("YR"), v("pX", 0, 64))
+            dma("A", hbm(T.yr[:]), v("YR"))
             break
 
         so = "S%d" % (rnd + 2)
-        nsc, nwk = "SC%d" % (rnd + 2), "WK%d" % (rnd + 2)
-        fin()
-        tt(v(so, 0, 512), ind(v(ht), v("QL")), v("O2S"), ADD)
-        act(v("SBR"), ind(v("SCN"), v("QL")))
-        send("a%d" % (rnd + 1), v(so, 0, 512), nwk)
-        mms(v("pX"), [(v("A45"), v("S1", 512, 1024)), (v("WQ"), v(so, 0, 512)), (v("A03"), v("SBR"))])
-        act(v(so, 512, 1024), v("pX"))
-        send("b%d" % (rnd + 1), v(so, 512, 1024), nsc)
-
+        nsc, nwk, ntb = "SC%d" % (rnd + 2), "WK%d" % (rnd + 2), "TB%d" % (rnd + 2)
+        xb = ("pE0", "pK")
+        nu = 1.0 / 256 if rnd else 1.0
+        mm(v("pX"), IDB, ghost("NUM"), True, False)
+        mms(v("pE1"), [(v("A67"), v("S1", 512, 1024))] + ([(v("WQ0"), v("S2", 0, 512))] if rnd else []))
+        for h in range(2):
+            mm(v("pY%d" % h), v("A67"), part("SC1", 512, h), True, False)
+            if rnd == 0 or h == 1:
+                mm(v(xb[h]), IDB, part("PHI", 512, h), True, False)
         if rnd == 1:
-            tt(PB, PA, RT, MUL)
-            tt(v("LE", 0, 128, 2), PB, XN2, ADD)
-            tt(v("LH", 1, 128, 2), PB, XN2, ADD)
-            t_to_list("LE", "LH", 320)
-            ts(IY, RT, 1536.0, MUL, -1536.0, ADD)
-            ts(v("CP", 192, 256), RT, 0.75 * BIG, MUL, -0.25 * BIG, ADD)
-            tt(SD, v("LE", 0, 128, 2), IY, ADD)
-            ts(v("WN"), v("pW", 320, 384), 1023.0, MIN)
-            cp(v("YL"), v("pW", 320, 384))
-            mm(v("pW", 384, 448), v("PERM"), v("WN"))
-        else:
-            ts(v("IDS"), v("IDB"), 1.0 / 256, MUL)
-        act(own("RR"), ind(v("P2R"), v("P2L")))
+            for b in range(8):
+                mm(v("pE0", b, 512, 8), v("NBS", b, 1024, 8), part("RNB", 64, 0))
+            for b in range(8):
+                mm(v("pD", 40 * b, 40 * b + 40), v("NBS", b, 1024, 8), part("RD", 40, 0))
         tt(v("KB"), ind(v("O2"), v("P2L")), v("O2B"), ADD)
-        if rnd == 1:
-            cp(v("SL"), v("pW", 384, 448))
-        for h in range(2):
-            mms(v("pY%d" % h), [(v("IDS"), part("PHI", 512, h)), (v("IDB"), part("KB", 512, h))])
-        arrive("a%d" % (rnd + 1), nwk)
-        mms(v("pX"), [(v("IDS"), ghost("PHI")), (v("IDB"), ghost(nwk))])
+        act(v("RR"), ind(v("P2R"), v("P2L")))
         if rnd == 0:
-            ts(JN, CA, DEF1, GE)
-            cp(IY, v("pU", 0, 64))
-            tt(v("pU", 320, 384), XN, v("pU", 64, 128), SUB)
-            tt(RT, JN, TT, AL.is_gt)
-            tt(v("pU", 256, 320), v("pU", 128, 192), IY, SUB)
-            ts(v("CP", 192, 256), RT, 1.75 * BIG, MUL, -0.25 * BIG, ADD)
+            cp(v(so, 0, 512), ind(v("KB"), v("SNL")))
+        else:
+            tt(v(so, 0, 512), ind(v("KB"), v("SNL")), v("S2", 0, 512), SUB)
+        mul(v("SBR"), ind(v("RR"), v("SNL")), pc(12))
+        send("a%d" % (rnd + 1), v(so, 0, 512), nwk)
+        fin = to_list("RR", "RL", 448)
         for h in range(2):
-            (cp if rnd == 0 else act)(part("YT", 512, h), v("pY%d" % h))
-        act(ghost("XT"), v("pX"))
-        if rnd == 0:
-            mul(v("WB", 64, 128), v("WB", 0, 64), BIG / BIG1)
-            mul(pc(21), pc(19), BIG)
-            lin(XN2, XN, 1.0, 1536.0)
-        fin = to_list("RR", 64, "RL", 448)
-        if rnd == 1:
-            neighbours_a("SL")
-        for h in range(2):
-            mms(v("pY%d" % h), [(v("A45"), part("SC1", 512, h)), (v("WQ"), part("KB", 512, h))], True, False)
+            mm(v("pY%d" % h), v("WQ0"), part("KB", 512, h), False, True)
+        mm(v("pX"), v("WQ0"), v(so, 0, 512), False, True)
         fin()
-
-        arrive("b%d" % (rnd + 1), nsc)
-        dma("S", ghost("SCN"), ghost(nsc))
-        dma("S", ghost("HT"), ghost(nwk))
         if rnd == 1:
-            act(v("YSG"), ind(own("YT"), v("SL")))
-            fin = neighbours_b("NL3", lambda: None)
-        tt(own("XT"), ind(v(nwk), v("RL")), own("YT"), ADD)
+            masked("pE0", range(3))
+        tt(v(so, 512, 1024), v("pX"), v("SBR"), ADD)
+        send("b%d" % (rnd + 1), v(so, 512, 1024), ntb)
+        if rnd == 1:
+            masked("pE0", [3])
+            mm(v(xb[1]), IDB, part("KB", 512, 1), False, False)
+            fin = nb_lists("NL3")
+            mms(v(xb[0]), [(IDB, part("PHI", 512, 0)), (IDB, part("KB", 512, 0))], True, False)
+        else:
+            for h in range(2):
+                mm(v(xb[h]), IDB, part("KB", 512, h), False, False)
+        tt(v(so, 1024, 1536), v("pE1"), v(so, 512, 1024), ADD)
+        send("c%d" % (rnd + 1), v(so, 1024, 1536), nsc)
+        if rnd == 1:
+            iota(ghost("OT"), [[0, 512]], int(LIFT / 256), 0)
+        act(part("ST", 512, 0), v("pY0"))
+        act(part("ST", 512, 1), v("pY1"))
+        mms(v("pX"), [(IDB, ghost("PHI"))] + [(IDB, ghost("WK2"))] * rnd, True, False)
         if rnd == 1:
             fin()
-            cp(IY, v("pU", 0, 64))
-            tt(v("pU", 320, 384), SD, v("pU", 64, 128), SUB)
-            tt(v("pU", 256, 320), v("pU", 128, 192), IY, SUB)
+            default(v("SS"))
+        else:
+            ts(pc(30), pc(4), 8.0, MUL)
+            ts(v("WMF"), v("WM"), 256.0, MUL)
+            ts(v("GY"), v("ROW", 0, 8), pc(30), ADD)
+
+        arrive("a%d" % (rnd + 1), nwk)
+        mm(v("pX"), IDB, ghost(nwk), False, True)
+        ts(part("XT", 512, 4), v("pX"), nu, MUL)
+        if rnd == 0:
+            ts(v("ZB"), v("ROW"), pc(24), EQ, pc(17), MUL)
         for h in range(2):
-            act(part("TMP", 512, h), ind(v(nsc), part("RL", 32, h)))
-            mm(v("pY%d" % h), v("A09"), part("TMP", 512, h), False, True)
+            act(part("DG", 512, h), ind(v(nwk), part("RL", 32, h)))
+            mm(v(xb[h]), IDB, part("DG", 512, h), False, True)
+        arrive("b%d" % (rnd + 1), ntb)
+        dma("S", ghost("PR"), ghost(ntb))
+        dma("S", ghost("P2R"), ghost(ntb))
+        tt(own(nsc), ind(v(ntb), v("RL")), v("ST"), ADD)
         for h in range(2):
-            act(part("SCN", 512, h), v("pY%d" % h))
+            mul(part("XT", 512, 2 + h), v(xb[h]), nu)
+        arrive("c%d" % (rnd + 1), nsc)
 
     _emit(g, T, ops)

@@ -6,20 +6,19 @@ for _d, _l in (
     (U16, "SNL 32 NL1 256 NL3 256 UL 64 PL 64 P2L 64 RL 64 YL 64 GL 8 GY 8"),
     (I32, "SNI 32 NBQ 256 NBI 2048 PI 16"),
     (F16, "NBH 256 NBS 1024 LM 512 LH 128 LY 128 M2 4096"),
-    (H16, "PHI 1536 PH2 1024 HI 1024 HS 512 NUM 1536 SC1 1536 SC2 1536 SC3 1536 TB2 1536 TB3 1536 ST 1024 DG 1024 "
+    (H16, "PHI 1536 PH2 1024 HI 1024 HS 512 NUM 1536 NG 512 SC1 1536 SC2 1536 SC3 1536 TB3 1536 ST 1024 DG 1024 "
           "WK2 1536 WK3 1536 RR 1024 PR 1536 P2R 1536 OT 1536 OB 1024 O2 1536 O2B 1024 KB 1024 SBR 512 S1 1024 "
           "S2 1536 S3 1536 M1 4096 KG 4096 BF 1024 PEN 256 DEFT 320"),
     (F, "YP 1024 XS 1024 XT 2560 M3 4096 YK 1024 YR 64 KEEP 320 RM 320 ZZ 320 RESET 320 YY 64 SS 64"),
-    (H16, "MK 128 RNB 256 RD 160 R2 64 IDB 128 Z 144 ZB 144 W4 128 W5 128 W5N 128 A67 128 WQ0 128 "
-          "WM 8 WS 8 WE 64"),
-    (F, "PC 48 ROW 144 GB 192 OH 16 STB 12 ONE 160 RDT 160 RDU 160 MKI 128 WA 128 WMF 8 XN 64"),
+    (H16, "MK 128 MKW 512 RNB 256 RD 160 R2 64 IDB 128 IDS 128 Z 144 ZB 144 W5 256 A67 128 WQ0 128 WM 8 WS 8 WE 64"),
+    (F, "PC 48 ROW 256 BLK 8 GB 16 OH 16 STB 12 ONE 160 RDT 160 RDU 160 MKI 128 WA 128 WMF 8 XN 64"),
 ):
     _w = _l.split()
     for _k in range(0, len(_w), 2):
         SCRATCH[_w[_k]] = ("sbuf", [128, int(_w[_k + 1])], _d)
 for _n in ("pK", "pD", "pE0", "pE1", "pW", "pX", "pY0", "pY1"):
     SCRATCH[_n] = ("psum", [128, 512], F)
-SEMAPHORES = ["cV", "cA", "cP", "cG", "sent", "a0", "a1", "a2", "b0", "b1", "b2", "c1", "c2"] + ["d%d" % k for k in range(30)]
+SEMAPHORES = ["cV", "cA", "cP", "cG", "sent", "a0", "a1", "a2", "b0", "b1", "b2", "c1", "c2"] + ["d%d" % k for k in range(44)]
 
 AL = AluOpType
 AF = ActivationFunctionType
@@ -28,7 +27,8 @@ BIG = float(2 ** 22)
 HUGE = 1e12
 LIFT = 49152.0
 ROUND16 = 1.5 * 2 ** 27
-VH = (384, 256, 256)
+NC = 20
+VH = (512, 288, 192)
 
 
 def _emit(g, T, ops):
@@ -195,10 +195,10 @@ def rank_program(g, core, T, topo):
     def arrive(sem, dst):
         rec("X", None, [v(dst, 1024, 1536)], [], own=(sem, len(topo.engines(prv, core))))
 
-    def to_list(src, dst, col):
+    def to_list(src, dst, col, a=0, b=64, bank="pW"):
         for i in range(16):
-            mm(v("pW", col, col + 64), v("Z", 15 - i, 143 - i), v(src, i, 1024, 16), i == 0, i == 15)
-        return lambda: cp(v(dst), v("pW", col, col + 64))
+            mm(v(bank, col + a, col + b), v("Z", 15 - i, 143 - i), v(src, 16 * a + i, 16 * b, 16), i == 0, i == 15)
+        return lambda: cp(v(dst, a, b), v(bank, col + a, col + b))
 
     def own(name):
         return v(name, 0, 1024)
@@ -209,68 +209,67 @@ def rank_program(g, core, T, topo):
     def at(name, pos):
         return v(name, pos, 320, 5)
 
-    row = v("ROW", 0, 128)
-    IDB = v("IDB")
+    def band(dst, src, lo, hi, n):
+        tmp = v("WA", 0, 8 * n)
+        asel(tmp, src, [[0, n], [-16, 8]], -lo, 1, GE)
+        asel(dst, tmp, [[0, n], [16, 8]], hi, -1, GE)
 
-    AND, SHR = AL.bitwise_and, AL.logical_shift_right
+    IDB = v("IDB")
+    ones = v("ONE", 0, 8)
+
+    AND = AL.bitwise_and
     p = v("PI", 0, 1)
+    dma("A", v("NBQ"), hbm(T.nb[:]))
     dma("S", v("SNI"), hbm(T.snd[:]))
-    dma("A", own("PHI"), hbm(T.phi[:]))
-    dma("S", v("NBQ"), hbm(T.nb[:]))
+    dma("S", own("PHI"), hbm(T.phi[:]))
     iota(p, [[0, 1]], 0, 1, False)
-    iota(v("ROW"), [[1, 144]], 0, 0)
+    iota(v("ROW"), [[1, 256]], 0, 0)
+    iota(v("GB", 0, 6), [[256, 6]], 0, 0)
     ms(v("ONE"), 1.0)
-    ms(v("DEFT"), 0.0)
     ts(v("PI", 1, 2), p, 15, AND)
-    ts(v("PI", 2, 3), p, 4, SHR)
+    ts(v("PI", 2, 3), p, 4, AL.logical_shift_right)
     ts(v("PI", 3, 4), p, 1, AND)
     ts(v("PI", 4, 5), p, 7, AND)
-    ts(v("PI", 5, 6), p, 3, SHR, 1, AND)
-    ts(v("PI", 6, 7), p, 1, SHR)
-    cp(v("PC", 0, 7), v("PI", 0, 7))
-    iota(v("GB", 128, 192), [[4, 4], [16, 8], [0, 2]], 0, 0)
-    iota(v("MKI"), [[0, 8], [1, 2], [0, 8]], 0, 0)
-    iota(v("GB", 0, 64), [[0, 8], [1, 8]], 0, 0)
-    iota(v("GB", 64, 128), [[1, 8], [0, 8]], 0, 0)
+    cp(v("PC", 0, 5), v("PI", 0, 5))
     ts(v("OH"), v("ROW", 0, 16), pc(1), EQ)
-    ts(pc(11), pc(2), 16.0, MUL, 6.0, ADD)
-    ts(pc(9), oh(4), float(rank), MUL, oh(5), ADD)
-    ts(pc(7), oh(0), oh(2), ADD)
-    ts(pc(8), oh(1), oh(3), ADD)
-    ts(v("STB", 0, 8), v("ROW", 0, 8), pc(7), MUL, pc(9), ADD)
-    for h in range(8):
-        lin(part("NUM", 128, h), row, pc(8), part("STB", 1, h))
+    ts(pc(31), oh(0), 8.0, MUL, oh(4), ADD)
+    ts(pc(9), oh(2), float(rank), MUL, oh(3), ADD)
+    ts(pc(8), oh(1), 8.0, MUL, oh(5), ADD)
+    ts(v("STB", 0, 4), v("GB", 0, 4), pc(31), MUL, pc(9), ADD)
+    mul(v("W5"), v("ROW"), 0.0)
+    for h in range(4):
+        lin(part("NUM", 256, h), v("ROW"), pc(8), part("STB", 1, h))
     for q in range(4):
-        ts(part("RNB", 64, q), v("GB", 128, 192), float(q), ADD, pc(0), EQ)
-    ts(v("STB", 8, 12), v("ROW", 8, 12), oh(0), MUL)
-    ts(pc(10), pc(1), 2.0, GE)
-    ts(v("W4"), row, pc(11), EQ, 1.0 / 16, MUL)
-    ts(v("W5"), row, -1.0, ADD, pc(11), EQ)
-    ts(pc(12), pc(1), 5.0, AL.is_le, pc(10), MUL)
+        asel(part("RNB", 64, q), v("ONE", 0, 64), [[-4, 4], [-16, 8], [0, 2]], -q, 1)
     asel(IDB, v("ONE", 0, 128), [[-1, 128]], 0, 1)
-    cp(v("SNL"), v("SNI"))
-    dma("S", v("PH2"), own("PHI"))
-    tt(v("W5N"), v("W4"), v("W5"), SUB)
+    iota(v("MKI"), [[0, 8], [1, 2], [0, 8]], 0, 0)
+    ts(pc(12), pc(1), 3.0, AL.is_le)
+    ts(v("BLK"), v("ROW", 0, 8), pc(2), EQ)
+    ts(v("STB", 4, 6), v("GB", 4, 6), oh(4), MUL)
     cp(v("NBH"), v("NBQ"))
+    cp(v("SNL"), v("SNI"))
+    cp(v("W5", 7, 128, 16), v("BLK"))
+    cp(v("W5", 134, 256, 16), v("BLK"))
+    ts(v("W5", 135, 256, 16), v("BLK"), -1.0, MUL)
+    dma("S", v("PH2"), own("PHI"))
     cp(v("S1", 0, 512), ind(own("PHI"), v("SNL")))
     mul(v("SBR"), ind(own("NUM"), v("SNL")), pc(12))
-    for h in range(8, 12):
-        lin(part("NUM", 128, h), row, oh(1), part("STB", 1, h))
     send("a0", v("S1", 0, 512), "PHI")
     ts(v("HS"), v("S1", 0, 512), ROUND16, ADD, -ROUND16, ADD)
+    W5, W5N = part("W5", 128, 0), part("W5", 128, 1)
     for q in range(4):
         for b in range(8):
             mm(v("pY1", b, 512, 8, rows=(32 * q, 32 * q + 32, 1)), v("NBH", b, 256, 8), part("RNB", 64, q))
-    mms(v("pX"), [(v("W5"), v("S1", 0, 512)), (IDB, v("SBR")), (v("W5N"), v("HS")), (IDB, ghost("NUM"))])
+    mm(v("pY0"), IDB, part("NUM", 512, 0), True, False)
+    mms(v("pX"), [(W5, v("S1", 0, 512)), (IDB, v("SBR")), (W5N, v("HS"))])
+    mm(v("pE0"), IDB, part("NUM", 512, 1), True, False)
+    for h in range(2):
+        lin(part("NG", 256, h), v("ROW"), oh(5), part("STB", 1, 4 + h))
     act(v("S1", 512, 1024), v("pX"))
     send("b0", v("S1", 512, 1024), "SC1")
+    tt(v("R2"), v("IDB", 0, 128, 2), v("IDB", 1, 128, 2), ADD)
     ts(v("MK"), v("MKI"), pc(3), EQ)
     ts(v("HI"), own("PHI"), ROUND16, ADD, -ROUND16, ADD)
-    ts(v("R2"), v("ROW", 0, 64), pc(6), EQ)
-
-    def masked(bank, ks):
-        for k in ks:
-            tt(part("LM", 128, k), part(bank, 128, k), v("MK"), MUL)
 
     def nb_lists(dst):
         for k in range(4):
@@ -278,50 +277,48 @@ def rank_program(g, core, T, topo):
         return lambda: cp(v(dst), v("pW", 0, 256))
 
     def own_pieces(h, bank):
-        mms(v(bank), [(IDB, part("NUM", 512, h)), (v("W5"), part("PHI", 512, h)), (v("W5N"), part("HI", 512, h))])
+        mms(v(bank), [(W5, part("PHI", 512, h)), (W5N, part("HI", 512, h))], False, True)
         act(part("SC1", 512, h), v(bank))
 
+    mul(v("WM"), v("BLK"), 2.0)
     own_pieces(0, "pY0")
-    masked("pY1", range(4))
+    for k in range(4):
+        tt(part("LM", 128, k), part("pY1", 128, k), v("MK"), MUL)
     fin = nb_lists("NL1")
     own_pieces(1, "pE0")
-    ts(pc(13), oh(6), -16.0, MUL, oh(7), SUB)
-    ts(pc(14), oh(8), oh(9), ADD)
-    ts(pc(15), oh(2), 1024.0, MUL, oh(4), ADD)
-    ts(pc(16), oh(5), 16384.0, MUL, pc(13), ADD)
-    ts(pc(17), oh(3), 8.0, MUL, pc(15), ADD)
-    fin()
-    ts(v("WM"), v("ROW", 0, 8), pc(2), EQ, 2.0, MUL)
+    ms(v("DEFT"), 16384.0)
     ms(at("DEFT", 4), BIG / 2)
+    fin()
+    iota(v("WA", 64, 128), [[-8, 8], [0, 8]], 0, 0)
+    asel(v("WA", 64, 128), v("WA", 64, 128), [[0, 8], [-16, 8]], -3, 1, EQ, 1.0)
+    band(v("WE"), v("WA", 64, 128), 0, 3, 8)
+    iota(v("WA", 64, 72), [[0, 8]], -1, 0)
+    band(v("WS"), v("WA", 64, 72), 6, 9, 1)
     pat = [[-1, 4], [-16, 8], [4, 5]]
     asel(v("RDT"), v("ONE"), pat, -12, 1)
     asel(v("RDU"), v("RDT"), pat, -8, 1, AL.not_equal, -1.0)
     asel(v("RD"), v("RDU"), [[-1, 4], [-16, 8], [0, 5]], 0, 1, GE)
     iota(v("XN"), [[1, 8], [0, 8]], 0, 8)
+    iota(v("GB", 8, 16), [[5, 8]], 4, 0)
     iota(v("RESET"), [[0, 320]], 0, 0)
-    iota(ghost("OT"), [[0, 512]], int(LIFT), 0)
-    col, loc = [[0, 8], [1, 16]], [[0, 8], [-1, 16]]
     asel(at("RESET", 0), at("RESET", 1), [[0, 64]], 0, 0, AL.not_equal, HUGE)
-    asel(v("A67"), IDB, col, -6, 0, GE)
-    asel(v("A67"), v("A67"), loc, 7, 0, GE)
+    asel(v("A67"), IDB, [[0, 8], [1, 16]], -6, 0, GE)
+    asel(v("A67"), v("A67"), [[0, 8], [-1, 16]], 7, 0, GE)
+    iota(ghost("OT"), [[0, 512]], int(LIFT), 0)
+    iota(v("Z"), [[0, 144]], 0, 0)
+    band(v("Z", 15, 143, 16), ones, 4, 5, 1)
     iota(ghost("O2"), [[0, 512]], 0, 0)
-    iota(own("WK2"), [[0, 1024]], 0, 0)
-    iota(v("NBI", 0, 1024), [[0, 1024]], 0, 0, False)
-    iota(v("NBI", 1024, 2048), [[0, 1024]], 0, 0, False)
+    iota(v("WQ0"), [[0, 128]], 0, 0)
+    for j in range(2):
+        band(v("WQ0", 8 + j, 128, 16), ones, 8 * j, 8 * j + 7, 1)
     arrive("a0", "PHI")
     arrive("b0", "SC1")
-    dma("S", ghost("PR"), ghost("SC1"))
-    dma("S", ghost("P2R"), ghost("SC1"))
-    dma("S", own("TB2"), own("NUM"))
-    dma("S", own("TB3"), own("NUM"))
-    dma("S", own("WK3"), own("WK2"))
-    dma("S", v("NBI", 0, 1024, rows=(0, 128, 4)), hbm(T.nb[:]))
-    dma("S", v("NBI", 1024, 2048, rows=(0, 128, 4)), hbm(T.nb[:]))
 
     def default(u):
         tt(at("pD", 3), at("pD", 3), u, SUB)
         cp(at("pD", 4), u)
 
+    xb = ("pE0", "pK")
     for rnd in range(3):
         nl = "NL3" if rnd == 2 else "NL1"
         mx = "M%d" % (rnd + 1)
@@ -354,134 +351,152 @@ def rank_program(g, core, T, topo):
                 mm(key(k, b), v("KG", a + b, a + 1024, 8), v("WS"), False, False)
 
         def pen(j, stop=False):
-            act(part("PEN", 128, j), v("pE%d" % j, 0, 128), AF.Relu, pc(20))
+            act(part("PEN", 128, j), v("pE%d" % j, 0, 128), AF.Relu, pc(20), BIG)
             return lambda: [mm(at("pK", 3 - k), IDB, part("PEN", 64, k), False, stop and k & 1 == 1) for k in (2 * j, 2 * j + 1)]
 
         mm(v("pK", 0, 320), IDB, v("DEFT"), True, False)
         vh = VH[rnd]
-        big(0)
-        if rnd == 0:
-            ts(pc(19), oh(5), -8.0, MUL)
-            ts(pc(18), pc(16), pc(14), SUB)
-            ts(v("WA", 64, 128), v("GB", 0, 64), pc(2), EQ, BIG, MUL)
-            ts(v("WA", 0, 64), v("GB", 64, 128), pc(19), MUL, pc(17), ADD)
-            ts(v("WS"), v("ROW", 0, 8), pc(2), EQ, pc(18), MUL)
-            ts(pc(20), pc(0), -64.0 * BIG, MUL, (1.0 - rank) * BIG, ADD)
-            tt(v("WE"), v("WA", 0, 64), v("WA", 64, 128), MUL)
-        small(0), big_mm(0), small_mm(0)
-        if rnd == 0:
-            for q in range(4):
-                for b in range(8):
-                    mm(v("pD", 40 * b, 40 * b + 40, rows=(32 * q, 32 * q + 32, 1)), v("NBH", b, 256, 8), part("RD", 40, q))
-        big(1), small(1), big_mm(1), small_mm(1)
-        if vh:
+        if rnd == 2:
             cp(v("KG", 4096 - vh, 4096), ind(kw, v(nl, 256 - vh // 16, 256)))
-        big(2), small(2)
-        f0 = pen(0)
-        small_mm(2), big_mm(2)
-        f0()
-        big(3), small(3, 1024 - vh)
+            small(3, 1024 - vh), small_mm(3)
+            for k in range(3):
+                big(k), small(k)
+                if k == 2:
+                    f0 = pen(0)
+                big_mm(k), small_mm(k)
+            f0()
+            big(3)
+            default(v("SS"))
+            f0 = pen(1, True)
+            big_mm(3)
+            f0()
+        else:
+            big(0), small(0), big_mm(0), small_mm(0)
+            if rnd == 0:
+                lin(pc(20), pc(0), -64.0 * BIG, (1.0 - rank) * BIG)
+                mul(pc(22), pc(4), 40.0)
+                mms(v("pY0"), [(IDB, v("NG")), (IDB, ghost("SC1"))])
+            big(1), small(1), big_mm(1), small_mm(1)
+            if rnd == 0:
+                for q in range(4):
+                    for b in range(8):
+                        mm(v("pD", 40 * b, 40 * b + 40, rows=(32 * q, 32 * q + 32, 1)), v("NBH", b, 256, 8), part("RD", 40, q))
+            cp(v("KG", 4096 - vh, 4096), ind(kw, v(nl, 256 - vh // 16, 256)))
+            big(2), small(2)
+            f0 = pen(0)
+            small_mm(2), big_mm(2)
+            f0()
+            big(3), small(3, 1024 - vh)
+            if rnd == 0:
+                default(v("XN"))
+                ts(v("GL"), v("GB", 8, 16), pc(22), ADD)
+            small_mm(3)
+            f0 = pen(1, True)
+            big_mm(3)
+            f0()
         if rnd == 0:
-            ts(pc(21), pc(4), 40.0, MUL, 4.0, ADD)
-            default(v("XN"))
-            ts(v("GL"), v("ROW", 0, 8), 5.0, MUL, pc(21), ADD)
-            ts(pc(24), pc(2), 16.0, MUL, 15.0, ADD)
-            ts(pc(25), oh(0), 128.0, MUL, oh(1), ADD)
-            ts(v("Z"), v("ROW"), pc(24), EQ, pc(25), MUL)
-        small_mm(3)
-        f0 = pen(1, True)
-        big_mm(3)
-        f0()
+            act(ghost("SC1"), v("pY0"))
+            dma("S", ghost("PR"), ghost("SC1"))
+            dma("S", ghost("P2R"), ghost("SC1"))
+            for j in range(4):
+                dma("S", part("WK%d" % (2 + (j >> 1)), 512, j & 1), ghost("O2"))
+            for j in range(4):
+                dma("S", part("MKW", 128, j), v("MK"))
+            dma("S", own("TB3"), own("NUM"))
         if rnd != 1:
             lin(v("YP"), mine, 1.0, (-0.5 - LIFT) / unit)
-        else:
-            act(own("XT"), own("PHI"))
 
         scan(v("RM"), v("RESET"), v("pK", 0, 320), MAX, MIN)
         tt(v("KEEP"), v("pK", 0, 320), v("RM"), AL.not_equal)
         scan(v("ZZ"), v("KEEP"), v("pD", 0, 320), MUL, ADD)
         tt(v("LH"), ind(v("ZZ"), v("GL")), v("MK"), MUL)
         mm(v("pW", 256, 320), v("LH"), v("R2"))
-        if rnd < 2:
+        e0, e1, e2 = v("pD", 320, 384), v("pD", 384, 448), v("pD", 448, 512)
+        if rnd == 0:
             ts(at("DEFT", 4), at("RM", 4), BIG / 2, GE, BIG / 2, MUL)
         if rnd == 1:
-            ts(v("pE0", 320, 384), at("RM", 3), 1.5 * BIG, LT, 2.0 / BIG, MUL)
+            ts(e0, at("RM", 4), BIG / 2, GE, 1.5 * BIG, MUL)
+            tt(e1, at("RM", 3), e0, LT)
         cp(v("UL"), v("pW", 256, 320))
-
-        tt(own("OT"), ind(xw, v("UL")), v("YP"), SUB)
-        act(own("PR"), ind(kw, v("UL")))
-        if rnd == 1:
-            lin(v("OB"), own("OT"), 1.0, -2 * LIFT)
-        else:
-            ts(v("OB"), own("OT"), -2 * LIFT / unit, ADD)
-        if rnd == 0:
-            pl = "UL"
-        else:
-            pl = "PL"
-            fin = to_list("PR", "PL", 0)
-            if rnd == 1:
-                e1, e2 = v("pE0", 384, 448), v("pE0", 448, 512)
-                tt(e1, v("pE0", 320, 384), at("DEFT", 4), MUL)
-                ts(v("YY"), at("DEFT", 4), 2048.0 / BIG, MUL)
-                tt(e2, e1, at("ZZ", 3), MUL)
-                tt(e1, e2, v("XN"), ADD)
-                tt(v("YY"), e1, v("YY"), ADD)
-                cp(v("SS"), e1)
-                tt(v("LY"), ind(v("YY"), v("GY")), v("MK"), MUL)
-            fin()
-            if rnd == 1:
-                mm(v("pW", 320, 384), v("LY"), v("R2"))
-        act(own("P2R"), ind(v("PR"), v(pl)))
-        if rnd == 0:
+        if rnd < 2:
+            mm(v("pX"), IDB, v("NG"), True, False)
             for h in range(2):
-                tt(part("O2", 512, h), ind(v("OT"), part(pl, 32, h)), part("OB", 512, h), ADD)
+                mm(v("pY%d" % h), v("A67"), part("SC1", 512, h), True, False)
+
+        def twice(h, pl):
+            tt(part("O2", 512, h), ind(v("OT"), part(pl, 32, h)), part("OB", 512, h), ADD)
+
+        def ahead():
+            mms(v("pE1"), [(v("A67"), v("S1", 512, 1024))] + ([(v("WQ0"), v("S2", 0, 512))] if rnd else []))
+            for h in range(2):
+                mm(v(xb[h]), IDB, part("PHI", 512, h), True, False)
+
+        if rnd < 2:
+            tt(own("OT"), ind(xw, v("UL")), v("YP"), SUB)
+            act(own("PR"), ind(kw, v("UL")))
+        if rnd == 0:
+            ts(v("OB"), own("OT"), -2 * LIFT, ADD)
+            ahead()
+            act(own("P2R"), ind(v("PR"), v("UL")))
+            fin = to_list("P2R", "P2L", 64)
+            for h in range(2):
+                twice(h, "UL")
                 (cp if h else act)(part("O2B", 512, h), part("O2", 512, h))
+            fin()
+        elif rnd == 1:
+            fin = to_list("PR", "PL", 0)
+            lin(v("OB"), own("OT"), 1.0, -2 * LIFT)
+            ts(e0, e0, 2048.0 / (3 * BIG), MUL)
+            tt(e2, e1, at("ZZ", 3), MUL)
+            tt(v("SS"), e2, v("XN"), ADD)
+            tt(v("YY"), e0, v("SS"), ADD)
+            tt(v("LY"), ind(v("YY"), v("GY")), v("MK"), MUL)
+            fin()
+            ts(at("DEFT", 4), at("RM", 4), BIG / 2, GE, BIG / 2, MUL)
+            mm(v("pW", 320, 384), v("LY"), v("R2"))
+            ahead()
+            act(own("P2R"), ind(v("PR"), v("PL")))
+            twice(0, "PL")
+            cp(v("YL"), v("pW", 320, 384))
+            twice(1, "PL")
+            fin = to_list("P2R", "P2L", 64)
+            cp(v("O2B"), own("O2"))
+            mul(v("XS", 0, 640), ind(v("XT", 0, 2048), v("YL", 0, 40)), 1.0 / 256)
+            fin()
         else:
-            tt(own("O2"), ind(v("OT"), v(pl)), v("OB"), ADD)
-            if rnd == 1:
-                dma("S", v("O2B"), own("O2"))
-                cp(v("YL"), v("pW", 320, 384))
-            else:
-                cp(v("O2B"), own("O2"))
-        fin = to_list("P2R", "P2L", 64)
-        if rnd == 1:
-            mul(v("XS"), ind(v("XT", 0, 2048), v("YL")), 1.0 / 256)
-            cp(v("NBS"), ind(v("NBI"), v("YL")))
-        if rnd == 0:
-            ts(pc(29), pc(2), 16.0, MUL, pc(5), ADD)
-        fin()
-        if rnd == 0:
-            ts(v("WQ0"), row, -8.0, ADD, pc(29), EQ)
-
-        if rnd == 2:
-            cuts = (0, 56, 64)
+            fin = []
             for h in range(2):
-                a, b = cuts[h], cuts[h + 1]
-                act(v("BF", 16 * a, 16 * b), ind(v("P2R"), v("P2L", a, b)))
-                for i in range(a // 4, b // 4):
-                    mm(v("pX", 0, 64), v("ZB", 15 - i, 143 - i), part("BF", 64, i), i == 0, i == 15)
-            for h in range(4):
-                tt(part("YK", 256, h), ind(v("O2"), part("P2L", 16, h)), part("O2B", 256, h), ADD)
-                dma("S", hbm(T.yk[:, 256 * h:256 * h + 256]), part("YK", 256, h))
+                tt(part("OT", 512, h), ind(xw, part("UL", 32, h)), part("YP", 512, h), SUB)
+                act(part("PR", 512, h), ind(kw, part("UL", 32, h)))
+                fin.append(to_list("PR", "PL", 0, 32 * h, 32 * h + 32, "pY%d" % h))
+                if h == 0:
+                    lin(part("OB", 512, 0), part("OT", 512, 0), 1.0, -2 * LIFT / unit)
+            for h in range(2):
+                if h:
+                    ts(part("OB", 512, 1), part("OT", 512, 1), -2 * LIFT / unit, ADD)
+                fin[h]()
+                twice(h, "PL")
+                act(part("P2R", 512, h), ind(v("PR"), part("PL", 32, h)))
+                fin.append(to_list("P2R", "P2L", 0, 32 * h, 32 * h + 32, "pE%d" % h))
+            cp(part("O2B", 512, 0), part("O2", 512, 0))
+            act(part("O2B", 512, 1), part("O2", 512, 1))
+            fin[2]()
+            for h, (a, b) in enumerate(((0, 24), (24, 48), (48, 64))):
+                if h == 1:
+                    fin[3]()
+                if h < 2:
+                    for c, d in (((0, 32),), ((32, 52), (52, 64)))[h]:
+                        act(v("BF", 16 * c, 16 * d), ind(v("P2R"), v("P2L", c, d)))
+                        for i in range(c // 4, d // 4):
+                            mm(v("pX", 0, 64), v("ZB", 15 - i, 143 - i), part("BF", 64, i), i == 0, i == 15)
+                tt(v("YK", 16 * a, 16 * b), ind(v("O2"), v("P2L", a, b)), v("O2B", 16 * a, 16 * b), ADD)
+                dma("S", hbm(T.yk[:, 16 * a:16 * b]), v("YK", 16 * a, 16 * b))
             act(v("YR"), v("pX", 0, 64))
             dma("A", hbm(T.yr[:]), v("YR"))
             break
 
         so = "S%d" % (rnd + 2)
-        nsc, nwk, ntb = "SC%d" % (rnd + 2), "WK%d" % (rnd + 2), "TB%d" % (rnd + 2)
-        xb = ("pE0", "pK")
-        nu = 1.0 / 256 if rnd else 1.0
-        mm(v("pX"), IDB, ghost("NUM"), True, False)
-        mms(v("pE1"), [(v("A67"), v("S1", 512, 1024))] + ([(v("WQ0"), v("S2", 0, 512))] if rnd else []))
-        for h in range(2):
-            mm(v("pY%d" % h), v("A67"), part("SC1", 512, h), True, False)
-            if rnd == 0 or h == 1:
-                mm(v(xb[h]), IDB, part("PHI", 512, h), True, False)
-        if rnd == 1:
-            for b in range(8):
-                mm(v("pE0", b, 512, 8), v("NBS", b, 1024, 8), part("RNB", 64, 0))
-            for b in range(8):
-                mm(v("pD", 40 * b, 40 * b + 40), v("NBS", b, 1024, 8), part("RD", 40, 0))
+        nsc, nwk, ntb = "SC%d" % (rnd + 2), "WK%d" % (rnd + 2), ("NUM", "TB3")[rnd]
         tt(v("KB"), ind(v("O2"), v("P2L")), v("O2B"), ADD)
         act(v("RR"), ind(v("P2R"), v("P2L")))
         if rnd == 0:
@@ -490,52 +505,67 @@ def rank_program(g, core, T, topo):
             tt(v(so, 0, 512), ind(v("KB"), v("SNL")), v("S2", 0, 512), SUB)
         mul(v("SBR"), ind(v("RR"), v("SNL")), pc(12))
         send("a%d" % (rnd + 1), v(so, 0, 512), nwk)
-        fin = to_list("RR", "RL", 448)
         for h in range(2):
             mm(v("pY%d" % h), v("WQ0"), part("KB", 512, h), False, True)
         mm(v("pX"), v("WQ0"), v(so, 0, 512), False, True)
-        fin()
+        fin = to_list("RR", "RL", 448)
         if rnd == 1:
-            masked("pE0", range(3))
+            cp(v("NBS", 0, 16 * NC), ind(v("NBI"), v("YL", 0, NC)))
+        else:
+            ts(pc(30), pc(4), 8.0, MUL)
+            ts(v("GY"), v("ROW", 0, 8), pc(30), ADD)
         tt(v(so, 512, 1024), v("pX"), v("SBR"), ADD)
         send("b%d" % (rnd + 1), v(so, 512, 1024), ntb)
+        fin()
+        act(part("ST", 512, 0), v("pY0"))
+        act(part("ST", 512, 1), v("pY1"))
         if rnd == 1:
-            masked("pE0", [3])
-            mm(v(xb[1]), IDB, part("KB", 512, 1), False, False)
-            fin = nb_lists("NL3")
-            mms(v(xb[0]), [(IDB, part("PHI", 512, 0)), (IDB, part("KB", 512, 0))], True, False)
-        else:
-            for h in range(2):
-                mm(v(xb[h]), IDB, part("KB", 512, h), False, False)
+            cp(v("NBS", 16 * NC, 1024), ind(v("NBI"), v("YL", NC, 64)))
+            mul(v("XS", 640, 1024), ind(v("XT", 0, 2048), v("YL", 40, 64)), 1.0 / 256)
         tt(v(so, 1024, 1536), v("pE1"), v(so, 512, 1024), ADD)
         send("c%d" % (rnd + 1), v(so, 1024, 1536), nsc)
         if rnd == 1:
             iota(ghost("OT"), [[0, 512]], int(LIFT / 256), 0)
-        act(part("ST", 512, 0), v("pY0"))
-        act(part("ST", 512, 1), v("pY1"))
-        mms(v("pX"), [(IDB, ghost("PHI"))] + [(IDB, ghost("WK2"))] * rnd, True, False)
-        if rnd == 1:
-            fin()
-            default(v("SS"))
         else:
-            ts(pc(30), pc(4), 8.0, MUL)
-            ts(v("WMF"), v("WM"), 256.0, MUL)
-            ts(v("GY"), v("ROW", 0, 8), pc(30), ADD)
+            asel(v("IDS"), v("O2", 1024, 1152), [[-1, 128]], 0, 1, AL.not_equal, 1.0 / 256)
+            iota(v("WA", 64, 72), [[0, 8]], 512, 0)
+            band(v("WMF"), v("WA", 64, 72), 0, 15, 1)
+            asel(own("XT"), own("PHI"), [[0, 1024]], 0, 0)
+            iota(v("ZB"), [[0, 144]], 0, 0)
+            band(v("ZB", 15, 143, 16), ones, 0, 2, 1)
+        mm(v(xb[0]), IDB, part("KB", 512, 0), False, False)
 
         arrive("a%d" % (rnd + 1), nwk)
-        mm(v("pX"), IDB, ghost(nwk), False, True)
-        ts(part("XT", 512, 4), v("pX"), nu, MUL)
-        if rnd == 0:
-            ts(v("ZB"), v("ROW"), pc(24), EQ, pc(17), MUL)
+        if rnd:
+            mms(v("pX"), [(v("IDS"), ghost("PHI")), (v("IDS"), ghost("WK2")), (v("IDS"), ghost(nwk))])
+            for b in range(8):
+                mm(v("pD", b, 512, 8), v("NBS", b, 1024, 8), part("RNB", 64, 0))
+        else:
+            mms(v("pX"), [(IDB, ghost("PHI")), (IDB, ghost(nwk))])
+        mm(v(xb[1]), IDB, part("KB", 512, 1), False, False)
+        if rnd:
+            tt(v("LM"), v("pD"), v("MKW"), MUL)
         for h in range(2):
-            act(part("DG", 512, h), ind(v(nwk), part("RL", 32, h)))
+            (cp if rnd == 0 and h else act)(part("DG", 512, h), ind(v(nwk), part("RL", 32, h)))
+            if h:
+                act(part("XT", 512, 4), v("pX"))
             mm(v(xb[h]), IDB, part("DG", 512, h), False, True)
+            if rnd == 1 and h == 0:
+                fin = nb_lists("NL3")
+        if rnd == 1:
+            for b in range(8):
+                mm(v("pD", 40 * b, 40 * b + 40), v("NBS", b, 1024, 8), part("RD", 40, 0))
         arrive("b%d" % (rnd + 1), ntb)
         dma("S", ghost("PR"), ghost(ntb))
         dma("S", ghost("P2R"), ghost(ntb))
+        if rnd == 0:
+            for j in range(8):
+                dma("S", v("NBI", 1024 * (j & 1), 1024 * (j & 1) + 1024, rows=(j >> 1, 128, 4)), hbm(T.nb[:]))
         tt(own(nsc), ind(v(ntb), v("RL")), v("ST"), ADD)
+        if rnd == 1:
+            fin()
         for h in range(2):
-            mul(part("XT", 512, 2 + h), v(xb[h]), nu)
+            mul(part("XT", 512, 2 + h), v(xb[h]), 1.0 / 256 if rnd else 1.0)
         arrive("c%d" % (rnd + 1), nsc)
 
     _emit(g, T, ops)

from concourse.mybir import AluOpType, ActivationFunctionType

F, H16, I32, U16, F16 = "float32", "bfloat16", "int32", "uint16", "float16"
SCRATCH = {}
for _d, _l in (
    (U16, "SNL 32 NL1 256 NL3 256 UL 64 PL 64 P2L 64 RL 64 YL 64 GL 8 GY 8"),
    (I32, "SNI 32 NBQ 256 NBI 2048 PI 16"),
    (F16, "NBH 256 NBS 1024 LM 512 LH 128 LY 128 M2 4096"),
    (H16, "PHI 1536 PH2 1024 HI 1024 HS 512 NUM 1536 NG 512 SC1 1536 SC2 1536 SC3 1536 TB3 1536 ST 1024 DG 1024 "
          "WK2 1536 WK3 1536 RR 1024 PR 1536 P2R 1536 OT 1536 OB 1024 O2 1536 O2B 1024 KB 1024 SBR 512 S1 1024 "
          "S2 1536 S3 1536 M1 4096 KG 4096 BF 1024 PEN 256 DEFT 320"),
    (F, "YP 1024 XS 1024 XT 2560 M3 4096 YK 1024 YR 64 KEEP 320 RM 320 ZZ 320 RESET 320 YY 64 SS 64"),
    (H16, "MK 128 MKW 512 RNB 256 RD 160 R2 64 IDB 128 IDS 128 Z 144 ZB 144 W5 256 A67 128 WQ0 128 WM 8 WS 8 WE 64"),
    (F, "PC 48 ROW 256 BLK 8 GB 16 OH 16 STB 12 ONE 160 RDT 160 RDU 160 MKI 128 WA 128 WMF 8 XN 64"),
):
    _w = _l.split()
    for _k in range(0, len(_w), 2):
        SCRATCH[_w[_k]] = ("sbuf", [128, int(_w[_k + 1])], _d)
for _n in ("pK", "pD", "pE0", "pE1", "pW", "pX", "pY0", "pY1"):
    SCRATCH[_n] = ("psum", [128, 512], F)
SEMAPHORES = ["cV", "cA", "cP", "cG", "sent", "a0", "a1", "a2", "b0", "b1", "b2", "c1", "c2"] + ["d%d" % k for k in range(44)]

AL = AluOpType
AF = ActivationFunctionType
ADD, SUB, MUL, MAX, MIN, LT, GE, EQ = AL.add, AL.subtract, AL.mult, AL.max, AL.min, AL.is_lt, AL.is_ge, AL.is_equal
BIG = float(2 ** 22)
HUGE = 1e12
LIFT = 49152.0
ROUND16 = 1.5 * 2 ** 27
NC = 20
VH = (512, 288, 192)


def _emit(g, T, ops):
    queue = {"V": g.vector, "A": g.scalar, "P": g.tensor, "G": g, "S": g.sync}
    cnt = {"V": "cV", "A": "cA", "P": "cP", "G": "cG"}

    def meet(x, y):
        return x[0] == y[0] and x[1] < y[2] and y[1] < x[2]

    known = {q: {} for q in queue}
    clock, waits, used, touch = [], [], set(), {}
    for n, o in enumerate(ops):
        q = o["q"]
        if q == "X":
            clock.append({})
            waits.append([])
            touch.setdefault(o["w"][0][0], []).append(n)
            continue
        deps = []
        names = set(x[0] for x in o["r"] + o["w"])
        for m in sorted(set(m for x in names for m in touch.get(x, []))):
            p = ops[m]
            if p["q"] == "P" and q == "P":
                continue
            hit = any(meet(x, y) for x in o["r"] + o["w"] for y in p["w"]) or any(meet(x, y) for x in o["w"] for y in p["r"])
            if not hit and p["q"] != q:
                hit = any(x[0] == y[0] and x[0][0] == "p" for x in o["r"] + o["w"] for y in p["r"] + p["w"])
            if hit:
                deps.append(m)
        mine = []
        for m in reversed(deps):
            key = ops[m]["q"] if ops[m]["own"] is None else ("own", m)
            if known[q].get(key, -1) >= m:
                continue
            mine.append(m)
            used.add(m)
            known[q][key] = m
            for kk, vv in clock[m].items():
                if known[q].get(kk, -1) < vv:
                    known[q][kk] = vv
        waits.append(mine)
        for x in names:
            touch.setdefault(x, []).append(n)
        clock.append(dict(known[q]))
    val, num = {}, {q: 0 for q in cnt}
    for n, o in enumerate(ops):
        if o["own"] is not None:
            val[n] = o["own"]
        elif n in used:
            num[o["q"]] += 1
            val[n] = (cnt[o["q"]], num[o["q"]])
    for n, o in enumerate(ops):
        if o["q"] == "X":
            continue
        for m in waits[n]:
            queue[o["q"]].wait_ge(T.sem[val[m][0]], val[m][1])
        ins = o["f"]()
        if o["inc"] and n in val:
            ins.then_inc(T.sem[val[n][0]], 1 if o["own"] is None else 16)
    final = {}
    for n in val:
        final[val[n][0]] = max(final.get(val[n][0], 0), val[n][1])
    for s in final:
        g.wait_ge(T.sem[s], final[s])


def rank_program(g, core, T, topo):
    rank = T.rank_of(core)
    if rank is None:
        return
    nr = len(T.cores)
    nxt = T.cores[(rank + 1) % nr]
    prv = T.cores[(rank - 1) % nr]
    ops = []
    ndma = [0]
    nsent = [0]

    def v(name, a=0, b=None, s=1, rows=None):
        b = T[name].shape[1] if b is None else b
        ap = T[name][:, a:b:s] if rows is None else T[name][rows[0]:rows[1]:rows[2], a:b:s]
        return (ap, [(name, a, b)])

    def ind(win, off):
        return (win[0].indirect(off[0]), win[1] + off[1])

    def part(name, n, h):
        return v(name, n * h, n * h + n)

    def pc(k):
        return part("PC", 1, k)

    def oh(k):
        return part("OH", 1, k)

    def rec(q, f, w, r, own=None, inc=True):
        ops.append({"q": q, "f": f, "w": [x for a in w for x in a[1]], "r": [x for a in r for x in a[1]], "own": own, "inc": inc})

    def val(s):
        return s[0] if isinstance(s, tuple) else s

    def aps(*s):
        return [x for x in s if isinstance(x, tuple)]

    def cp(out, in_):
        rec("V", lambda: g.vector.tensor_copy(out[0], in_[0]), [out], [in_])

    def tt(out, a, b, op):
        rec("V", lambda: g.vector.tensor_tensor(out[0], a[0], b[0], op), [out], [a, b])

    def ts(out, a, s1, op0, s2=None, op1=None):
        if op1 is None:
            rec("V", lambda: g.vector.tensor_scalar(out[0], a[0], val(s1), None, op0), [out], [a] + aps(s1))
        else:
            rec("V", lambda: g.vector.tensor_scalar(out[0], a[0], val(s1), val(s2), op0, op1), [out], [a] + aps(s1, s2))

    def scan(out, a, b, op0, op1):
        rec("V", lambda: g.vector.tensor_tensor_scan(out[0], a[0], b[0], 0.0, op0, op1), [out], [a, b])

    def ms(out, c):
        rec("V", lambda: g.vector.memset(out[0], c), [out], [])

    def act(out, in_, func=AF.Copy, bias=0.0, scale=1.0):
        rec("A", lambda: g.scalar.activation(out[0], in_[0], func, bias=val(bias), scale=val(scale)), [out], [in_] + aps(bias, scale))

    def lin(out, in_, scale, bias):
        act(out, in_, AF.Identity, bias, scale)

    def mul(out, in_, scale):
        act(out, in_, AF.Copy, 0.0, scale)

    def mm(out, l, r, start=True, stop=True):
        rec("P", lambda: g.tensor.matmul(out[0], l[0], r[0], start, stop), [out], [l, r])

    def mms(out, pairs, start=True, stop=True):
        for j, (l, r) in enumerate(pairs):
            mm(out, l, r, start and j == 0, stop and j == len(pairs) - 1)

    def iota(out, pat, base, cm, flt=True):
        if flt:
            rec("G", lambda: g.iota(out[0], pat, base, cm, allow_small_or_imprecise_dtypes=True), [out], [])
        else:
            rec("G", lambda: g.iota(out[0], pat, base, cm), [out], [])

    def asel(out, in_, pat, base, cm, op=EQ, fill=0.0):
        rec("G", lambda: g.affine_select(out[0], in_[0], pat, op, fill, base, cm), [out], [in_])

    def dma(q, out, in_):
        e = g.sync if q == "S" else g.scalar
        s = "d%d" % ndma[0]
        ndma[0] += 1
        rec(q, lambda: e.dma_start(out[0], in_[0]), [out], [in_], own=(s, 16))

    def hbm(ap):
        return (ap, [])

    mask = topo.mask(core, nxt)
    rid, pid, _ = topo.addr(nxt)

    def send(sem, src, dst):
        nsent[0] += len(topo.engines(core, nxt))
        rec("G", lambda: g.remote_dma(T[dst][:, 1024:1536], src[0], T.sem[sem], T.sem["sent"], pid, rid, mask), [], [src],
            own=("sent", nsent[0]), inc=False)

    def arrive(sem, dst):
        rec("X", None, [v(dst, 1024, 1536)], [], own=(sem, len(topo.engines(prv, core))))

    def to_list(src, dst, col, a=0, b=64, bank="pW"):
        for i in range(16):
            mm(v(bank, col + a, col + b), v("Z", 15 - i, 143 - i), v(src, 16 * a + i, 16 * b, 16), i == 0, i == 15)
        return lambda: cp(v(dst, a, b), v(bank, col + a, col + b))

    def own(name):
        return v(name, 0, 1024)

    def ghost(name):
        return v(name, 1024, 1536)

    def at(name, pos):
        return v(name, pos, 320, 5)

    def band(dst, src, lo, hi, n):
        tmp = v("WA", 0, 8 * n)
        asel(tmp, src, [[0, n], [-16, 8]], -lo, 1, GE)
        asel(dst, tmp, [[0, n], [16, 8]], hi, -1, GE)

    IDB = v("IDB")
    ones = v("ONE", 0, 8)

    AND = AL.bitwise_and
    p = v("PI", 0, 1)
    dma("A", v("NBQ"), hbm(T.nb[:]))
    dma("S", v("SNI"), hbm(T.snd[:]))
    dma("S", own("PHI"), hbm(T.phi[:]))
    iota(p, [[0, 1]], 0, 1, False)
    iota(v("ROW"), [[1, 256]], 0, 0)
    iota(v("GB", 0, 6), [[256, 6]], 0, 0)
    ms(v("ONE"), 1.0)
    ts(v("PI", 1, 2), p, 15, AND)
    ts(v("PI", 2, 3), p, 4, AL.logical_shift_right)
    ts(v("PI", 3, 4), p, 1, AND)
    ts(v("PI", 4, 5), p, 7, AND)
    cp(v("PC", 0, 5), v("PI", 0, 5))
    ts(v("OH"), v("ROW", 0, 16), pc(1), EQ)
    ts(pc(31), oh(0), 8.0, MUL, oh(4), ADD)
    ts(pc(9), oh(2), float(rank), MUL, oh(3), ADD)
    ts(pc(8), oh(1), 8.0, MUL, oh(5), ADD)
    ts(v("STB", 0, 4), v("GB", 0, 4), pc(31), MUL, pc(9), ADD)
    mul(v("W5"), v("ROW"), 0.0)
    for h in range(4):
        lin(part("NUM", 256, h), v("ROW"), pc(8), part("STB", 1, h))
    for q in range(4):
        asel(part("RNB", 64, q), v("ONE", 0, 64), [[-4, 4], [-16, 8], [0, 2]], -q, 1)
    asel(IDB, v("ONE", 0, 128), [[-1, 128]], 0, 1)
    iota(v("MKI"), [[0, 8], [1, 2], [0, 8]], 0, 0)
    ts(pc(12), pc(1), 3.0, AL.is_le)
    ts(v("BLK"), v("ROW", 0, 8), pc(2), EQ)
    ts(v("STB", 4, 6), v("GB", 4, 6), oh(4), MUL)
    cp(v("NBH"), v("NBQ"))
    cp(v("SNL"), v("SNI"))
    cp(v("W5", 7, 128, 16), v("BLK"))
    cp(v("W5", 134, 256, 16), v("BLK"))
    ts(v("W5", 135, 256, 16), v("BLK"), -1.0, MUL)
    dma("S", v("PH2"), own("PHI"))
    cp(v("S1", 0, 512), ind(own("PHI"), v("SNL")))
    mul(v("SBR"), ind(own("NUM"), v("SNL")), pc(12))
    send("a0", v("S1", 0, 512), "PHI")
    ts(v("HS"), v("S1", 0, 512), ROUND16, ADD, -ROUND16, ADD)
    W5, W5N = part("W5", 128, 0), part("W5", 128, 1)
    for q in range(4):
        for b in range(8):
            mm(v("pY1", b, 512, 8, rows=(32 * q, 32 * q + 32, 1)), v("NBH", b, 256, 8), part("RNB", 64, q))
    mm(v("pY0"), IDB, part("NUM", 512, 0), True, False)
    mms(v("pX"), [(W5, v("S1", 0, 512)), (IDB, v("SBR")), (W5N, v("HS"))])
    mm(v("pE0"), IDB, part("NUM", 512, 1), True, False)
    for h in range(2):
        lin(part("NG", 256, h), v("ROW"), oh(5), part("STB", 1, 4 + h))
    act(v("S1", 512, 1024), v("pX"))
    send("b0", v("S1", 512, 1024), "SC1")
    tt(v("R2"), v("IDB", 0, 128, 2), v("IDB", 1, 128, 2), ADD)
    ts(v("MK"), v("MKI"), pc(3), EQ)
    ts(v("HI"), own("PHI"), ROUND16, ADD, -ROUND16, ADD)

    def nb_lists(dst):
        for k in range(4):
            mm(part("pW", 64, k), part("LM", 128, k), v("R2"))
        return lambda: cp(v(dst), v("pW", 0, 256))

    def own_pieces(h, bank):
        mms(v(bank), [(W5, part("PHI", 512, h)), (W5N, part("HI", 512, h))], False, True)
        act(part("SC1", 512, h), v(bank))

    mul(v("WM"), v("BLK"), 2.0)
    own_pieces(0, "pY0")
    for k in range(4):
        tt(part("LM", 128, k), part("pY1", 128, k), v("MK"), MUL)
    fin = nb_lists("NL1")
    own_pieces(1, "pE0")
    ms(v("DEFT"), 16384.0)
    ms(at("DEFT", 4), BIG / 2)
    fin()
    iota(v("WA", 64, 128), [[-8, 8], [0, 8]], 0, 0)
    asel(v("WA", 64, 128), v("WA", 64, 128), [[0, 8], [-16, 8]], -3, 1, EQ, 1.0)
    band(v("WE"), v("WA", 64, 128), 0, 3, 8)
    iota(v("WA", 64, 72), [[0, 8]], -1, 0)
    band(v("WS"), v("WA", 64, 72), 6, 9, 1)
    pat = [[-1, 4], [-16, 8], [4, 5]]
    asel(v("RDT"), v("ONE"), pat, -12, 1)
    asel(v("RDU"), v("RDT"), pat, -8, 1, AL.not_equal, -1.0)
    asel(v("RD"), v("RDU"), [[-1, 4], [-16, 8], [0, 5]], 0, 1, GE)
    iota(v("XN"), [[1, 8], [0, 8]], 0, 8)
    iota(v("GB", 8, 16), [[5, 8]], 4, 0)
    iota(v("RESET"), [[0, 320]], 0, 0)
    asel(at("RESET", 0), at("RESET", 1), [[0, 64]], 0, 0, AL.not_equal, HUGE)
    asel(v("A67"), IDB, [[0, 8], [1, 16]], -6, 0, GE)
    asel(v("A67"), v("A67"), [[0, 8], [-1, 16]], 7, 0, GE)
    iota(ghost("OT"), [[0, 512]], int(LIFT), 0)
    iota(v("Z"), [[0, 144]], 0, 0)
    band(v("Z", 15, 143, 16), ones, 4, 5, 1)
    iota(ghost("O2"), [[0, 512]], 0, 0)
    iota(v("WQ0"), [[0, 128]], 0, 0)
    for j in range(2):
        band(v("WQ0", 8 + j, 128, 16), ones, 8 * j, 8 * j + 7, 1)
    arrive("a0", "PHI")
    arrive("b0", "SC1")

    def default(u):
        tt(at("pD", 3), at("pD", 3), u, SUB)
        cp(at("pD", 4), u)

    xb = ("pE0", "pK")
    for rnd in range(3):
        nl = "NL3" if rnd == 2 else "NL1"
        mx = "M%d" % (rnd + 1)
        xw = v("PHI") if rnd == 0 else v("XT", 1024, 2560)
        kw = v("SC%d" % (rnd + 1))
        mine = v("XS") if rnd == 2 else v("PH2")
        wm = v("WMF") if rnd == 2 else v("WM")
        unit = 256.0 if rnd == 2 else 1.0

        def key(k, b):
            return v("pK", 40 * b + 3 - k, 40 * b + 40, 5)

        def big(k):
            tt(part(mx, 1024, k), ind(xw, part(nl, 64, k)), mine, MAX)

        def big_mm(k):
            for b in range(8):
                mm(key(k, b), v(mx, 1024 * k + b, 1024 * k + 1024, 8), wm, False, False)

        def small(k, n=1024):
            a = 1024 * k
            act(v("KG", a, a + n), ind(kw, v(nl, 64 * k, 64 * k + n // 16)))

        def small_mm(k):
            a = 1024 * k
            e0 = 64 * (k & 1)
            for b in range(8):
                mm(v("pE%d" % (k >> 1), e0 + 8 * b, e0 + 8 * b + 8), v("KG", a + b, a + 1024, 8), part("WE", 8, b))
            for b in range(8):
                mm(key(k, b), v("KG", a + b, a + 1024, 8), v("WS"), False, False)

        def pen(j, stop=False):
            act(part("PEN", 128, j), v("pE%d" % j, 0, 128), AF.Relu, pc(20), BIG)
            return lambda: [mm(at("pK", 3 - k), IDB, part("PEN", 64, k), False, stop and k & 1 == 1) for k in (2 * j, 2 * j + 1)]

        mm(v("pK", 0, 320), IDB, v("DEFT"), True, False)
        vh = VH[rnd]
        if rnd == 2:
            cp(v("KG", 4096 - vh, 4096), ind(kw, v(nl, 256 - vh // 16, 256)))
            small(3, 1024 - vh), small_mm(3)
            for k in range(3):
                big(k), small(k)
                if k == 2:
                    f0 = pen(0)
                big_mm(k), small_mm(k)
            f0()
            big(3)
            default(v("SS"))
            f0 = pen(1, True)
            big_mm(3)
            f0()
        else:
            big(0), small(0), big_mm(0), small_mm(0)
            if rnd == 0:
                lin(pc(20), pc(0), -64.0 * BIG, (1.0 - rank) * BIG)
                mul(pc(22), pc(4), 40.0)
                mms(v("pY0"), [(IDB, v("NG")), (IDB, ghost("SC1"))])
            big(1), small(1), big_mm(1), small_mm(1)
            if rnd == 0:
                for q in range(4):
                    for b in range(8):
                        mm(v("pD", 40 * b, 40 * b + 40, rows=(32 * q, 32 * q + 32, 1)), v("NBH", b, 256, 8), part("RD", 40, q))
            cp(v("KG", 4096 - vh, 4096), ind(kw, v(nl, 256 - vh // 16, 256)))
            big(2), small(2)
            f0 = pen(0)
            small_mm(2), big_mm(2)
            f0()
            big(3), small(3, 1024 - vh)
            if rnd == 0:
                default(v("XN"))
                ts(v("GL"), v("GB", 8, 16), pc(22), ADD)
            small_mm(3)
            f0 = pen(1, True)
            big_mm(3)
            f0()
        if rnd == 0:
            act(ghost("SC1"), v("pY0"))
            dma("S", ghost("PR"), ghost("SC1"))
            dma("S", ghost("P2R"), ghost("SC1"))
            for j in range(4):
                dma("S", part("WK%d" % (2 + (j >> 1)), 512, j & 1), ghost("O2"))
            for j in range(4):
                dma("S", part("MKW", 128, j), v("MK"))
            dma("S", own("TB3"), own("NUM"))
        if rnd != 1:
            lin(v("YP"), mine, 1.0, (-0.5 - LIFT) / unit)

        scan(v("RM"), v("RESET"), v("pK", 0, 320), MAX, MIN)
        tt(v("KEEP"), v("pK", 0, 320), v("RM"), AL.not_equal)
        scan(v("ZZ"), v("KEEP"), v("pD", 0, 320), MUL, ADD)
        tt(v("LH"), ind(v("ZZ"), v("GL")), v("MK"), MUL)
        mm(v("pW", 256, 320), v("LH"), v("R2"))
        e0, e1, e2 = v("pD", 320, 384), v("pD", 384, 448), v("pD", 448, 512)
        if rnd == 0:
            ts(at("DEFT", 4), at("RM", 4), BIG / 2, GE, BIG / 2, MUL)
        if rnd == 1:
            ts(e0, at("RM", 4), BIG / 2, GE, 1.5 * BIG, MUL)
            tt(e1, at("RM", 3), e0, LT)
        cp(v("UL"), v("pW", 256, 320))
        if rnd < 2:
            mm(v("pX"), IDB, v("NG"), True, False)
            for h in range(2):
                mm(v("pY%d" % h), v("A67"), part("SC1", 512, h), True, False)

        def twice(h, pl):
            tt(part("O2", 512, h), ind(v("OT"), part(pl, 32, h)), part("OB", 512, h), ADD)

        def ahead():
            mms(v("pE1"), [(v("A67"), v("S1", 512, 1024))] + ([(v("WQ0"), v("S2", 0, 512))] if rnd else []))
            for h in range(2):
                mm(v(xb[h]), IDB, part("PHI", 512, h), True, False)

        if rnd < 2:
            tt(own("OT"), ind(xw, v("UL")), v("YP"), SUB)
            act(own("PR"), ind(kw, v("UL")))
        if rnd == 0:
            ts(v("OB"), own("OT"), -2 * LIFT, ADD)
            ahead()
            act(own("P2R"), ind(v("PR"), v("UL")))
            fin = to_list("P2R", "P2L", 64)
            for h in range(2):
                twice(h, "UL")
                (cp if h else act)(part("O2B", 512, h), part("O2", 512, h))
            fin()
        elif rnd == 1:
            fin = to_list("PR", "PL", 0)
            lin(v("OB"), own("OT"), 1.0, -2 * LIFT)
            ts(e0, e0, 2048.0 / (3 * BIG), MUL)
            tt(e2, e1, at("ZZ", 3), MUL)
            tt(v("SS"), e2, v("XN"), ADD)
            tt(v("YY"), e0, v("SS"), ADD)
            tt(v("LY"), ind(v("YY"), v("GY")), v("MK"), MUL)
            fin()
            ts(at("DEFT", 4), at("RM", 4), BIG / 2, GE, BIG / 2, MUL)
            mm(v("pW", 320, 384), v("LY"), v("R2"))
            ahead()
            act(own("P2R"), ind(v("PR"), v("PL")))
            twice(0, "PL")
            cp(v("YL"), v("pW", 320, 384))
            twice(1, "PL")
            fin = to_list("P2R", "P2L", 64)
            cp(v("O2B"), own("O2"))
            mul(v("XS", 0, 640), ind(v("XT", 0, 2048), v("YL", 0, 40)), 1.0 / 256)
            fin()
        else:
            fin = []
            for h in range(2):
                tt(part("OT", 512, h), ind(xw, part("UL", 32, h)), part("YP", 512, h), SUB)
                act(part("PR", 512, h), ind(kw, part("UL", 32, h)))
                fin.append(to_list("PR", "PL", 0, 32 * h, 32 * h + 32, "pY%d" % h))
                if h == 0:
                    lin(part("OB", 512, 0), part("OT", 512, 0), 1.0, -2 * LIFT / unit)
            for h in range(2):
                if h:
                    ts(part("OB", 512, 1), part("OT", 512, 1), -2 * LIFT / unit, ADD)
                fin[h]()
                twice(h, "PL")
                act(part("P2R", 512, h), ind(v("PR"), part("PL", 32, h)))
                fin.append(to_list("P2R", "P2L", 0, 32 * h, 32 * h + 32, "pE%d" % h))
            cp(part("O2B", 512, 0), part("O2", 512, 0))
            act(part("O2B", 512, 1), part("O2", 512, 1))
            fin[2]()
            for h, (a, b) in enumerate(((0, 24), (24, 48), (48, 64))):
                if h == 1:
                    fin[3]()
                if h < 2:
                    for c, d in (((0, 32),), ((32, 52), (52, 64)))[h]:
                        act(v("BF", 16 * c, 16 * d), ind(v("P2R"), v("P2L", c, d)))
                        for i in range(c // 4, d // 4):
                            mm(v("pX", 0, 64), v("ZB", 15 - i, 143 - i), part("BF", 64, i), i == 0, i == 15)
                tt(v("YK", 16 * a, 16 * b), ind(v("O2"), v("P2L", a, b)), v("O2B", 16 * a, 16 * b), ADD)
                dma("S", hbm(T.yk[:, 16 * a:16 * b]), v("YK", 16 * a, 16 * b))
            act(v("YR"), v("pX", 0, 64))
            dma("A", hbm(T.yr[:]), v("YR"))
            break

        so = "S%d" % (rnd + 2)
        nsc, nwk, ntb = "SC%d" % (rnd + 2), "WK%d" % (rnd + 2), ("NUM", "TB3")[rnd]
        tt(v("KB"), ind(v("O2"), v("P2L")), v("O2B"), ADD)
        act(v("RR"), ind(v("P2R"), v("P2L")))
        if rnd == 0:
            cp(v(so, 0, 512), ind(v("KB"), v("SNL")))
        else:
            tt(v(so, 0, 512), ind(v("KB"), v("SNL")), v("S2", 0, 512), SUB)
        mul(v("SBR"), ind(v("RR"), v("SNL")), pc(12))
        send("a%d" % (rnd + 1), v(so, 0, 512), nwk)
        for h in range(2):
            mm(v("pY%d" % h), v("WQ0"), part("KB", 512, h), False, True)
        mm(v("pX"), v("WQ0"), v(so, 0, 512), False, True)
        fin = to_list("RR", "RL", 448)
        if rnd == 1:
            cp(v("NBS", 0, 16 * NC), ind(v("NBI"), v("YL", 0, NC)))
        else:
            ts(pc(30), pc(4), 8.0, MUL)
            ts(v("GY"), v("ROW", 0, 8), pc(30), ADD)
        tt(v(so, 512, 1024), v("pX"), v("SBR"), ADD)
        send("b%d" % (rnd + 1), v(so, 512, 1024), ntb)
        fin()
        act(part("ST", 512, 0), v("pY0"))
        act(part("ST", 512, 1), v("pY1"))
        if rnd == 1:
            cp(v("NBS", 16 * NC, 1024), ind(v("NBI"), v("YL", NC, 64)))
            mul(v("XS", 640, 1024), ind(v("XT", 0, 2048), v("YL", 40, 64)), 1.0 / 256)
        tt(v(so, 1024, 1536), v("pE1"), v(so, 512, 1024), ADD)
        send("c%d" % (rnd + 1), v(so, 1024, 1536), nsc)
        if rnd == 1:
            iota(ghost("OT"), [[0, 512]], int(LIFT / 256), 0)
        else:
            asel(v("IDS"), v("O2", 1024, 1152), [[-1, 128]], 0, 1, AL.not_equal, 1.0 / 256)
            iota(v("WA", 64, 72), [[0, 8]], 512, 0)
            band(v("WMF"), v("WA", 64, 72), 0, 15, 1)
            asel(own("XT"), own("PHI"), [[0, 1024]], 0, 0)
            iota(v("ZB"), [[0, 144]], 0, 0)
            band(v("ZB", 15, 143, 16), ones, 0, 2, 1)
        mm(v(xb[0]), IDB, part("KB", 512, 0), False, False)

        arrive("a%d" % (rnd + 1), nwk)
        if rnd:
            mms(v("pX"), [(v("IDS"), ghost("PHI")), (v("IDS"), ghost("WK2")), (v("IDS"), ghost(nwk))])
            for b in range(8):
                mm(v("pD", b, 512, 8), v("NBS", b, 1024, 8), part("RNB", 64, 0))
        else:
            mms(v("pX"), [(IDB, ghost("PHI")), (IDB, ghost(nwk))])
        mm(v(xb[1]), IDB, part("KB", 512, 1), False, False)
        if rnd:
            tt(v("LM"), v("pD"), v("MKW"), MUL)
        for h in range(2):
            (cp if rnd == 0 and h else act)(part("DG", 512, h), ind(v(nwk), part("RL", 32, h)))
            if h:
                act(part("XT", 512, 4), v("pX"))
            mm(v(xb[h]), IDB, part("DG", 512, h), False, True)
            if rnd == 1 and h == 0:
                fin = nb_lists("NL3")
        if rnd == 1:
            for b in range(8):
                mm(v("pD", 40 * b, 40 * b + 40), v("NBS", b, 1024, 8), part("RD", 40, 0))
        arrive("b%d" % (rnd + 1), ntb)
        dma("S", ghost("PR"), ghost(ntb))
        dma("S", ghost("P2R"), ghost(ntb))
        if rnd == 0:
            for j in range(8):
                dma("S", v("NBI", 1024 * (j & 1), 1024 * (j & 1) + 1024, rows=(j >> 1, 128, 4)), hbm(T.nb[:]))
        tt(own(nsc), ind(v(ntb), v("RL")), v("ST"), ADD)
        if rnd == 1:
            fin()
        for h in range(2):
            mul(part("XT", 512, 2 + h), v(xb[h]), 1.0 / 256 if rnd else 1.0)
        arrive("c%d" % (rnd + 1), nsc)

    _emit(g, T, ops)
